import numpy as np
import ml_dtypes


def mxq(x, axis, fmt="e4m3"):
    dtype, down = {"e4m3": (ml_dtypes.float8_e4m3fn, 7), "e5m2": (ml_dtypes.float8_e5m2, 14)}[fmt]
    v = np.moveaxis(np.asarray(x, np.float32).astype(ml_dtypes.bfloat16).astype(np.float64), axis, -1)
    blocks = v.reshape(v.shape[:-1] + (-1, 32))
    amax = np.abs(blocks).max(-1, keepdims=True)
    byte = np.maximum(np.where(amax > 0, np.frexp(amax)[1] - 1 + 127, 0) - down, 1)
    scale = np.exp2(byte - 127.0)
    codes = (blocks / scale).astype(np.float32).astype(dtype).astype(np.float64)
    return np.moveaxis((codes * scale).reshape(v.shape), -1, axis)


WIDE = False


def mx_kscale(k):
    if not WIDE:
        return np.ones(k)
    levels = np.array([10, -10, 5, -5, 0])
    if k % 512:
        return np.exp2(np.random.permutation(np.resize(levels, k // 32))).repeat(32)
    a = np.empty((k // 512, 16))
    for p in range(k // 512):
        a[p, :8] = np.random.permutation(np.resize(levels, 8))
        for g in range(8):
            far = levels[np.abs(levels - a[p, g]) >= 10]
            a[p, g + 8] = far[np.random.randint(len(far))]
    return np.exp2(a.ravel()).repeat(32)


def f64(x):
    return np.asarray(x).astype(np.float64)


def striped(idx):
    return np.tile(idx.reshape(-1, 16).T, (8, 1)).astype(np.uint16)


def unstriped(offs):
    return offs[:16].T.reshape(-1).astype(np.int64)


def relu(v):
    return np.maximum(v, 0.0)


K, T, E, C, H, N = 2048, 640, 4, 128, 512, 128


def by_expert(wq, xq):
    return np.concatenate([wq[e].T @ xq[:, e * C:(e + 1) * C] for e in range(E)], axis=1)


def setup_inputs():
    n = np.random.standard_normal
    s = mx_kscale(K)[:, None]
    u = mx_kscale(H)
    return {
        "xT": (n((K, T)) * s).astype(np.float32),
        "w1": (n((E, K, H)) / np.sqrt(K) / s[None]).astype(np.float32),
        "w3": (n((E, K, H)) / np.sqrt(K) / s[None] * u[None, None, :]).astype(np.float32),
        "w2": (n((E, H, N)) / np.sqrt(H) / u[None, :, None]).astype(np.float32),
        "gate": np.tile(np.random.uniform(0.2, 1.0, E * C), (N, 1)).astype(np.float32),
        "offs": striped(np.random.permutation(T)[:E * C]),
        "dst": striped(np.random.permutation(T)[:E * C]),
    }


def reference(xT, w1, w3, w2, gate, offs, dst):
    idx = unstriped(offs)
    xq = mxq(f64(xT)[:, idx], 0, "e4m3")
    h = relu(by_expert(mxq(f64(w1), 1, "e4m3"), xq))
    h = h * by_expert(mxq(f64(w3), 1, "e4m3"), xq)
    y = by_expert(mxq(f64(w2), 1, "e4m3"), mxq(h, 0, "e4m3"))
    out = np.zeros((N, T))
    out[:, unstriped(dst)] = f64(gate) * y
    return out

@@ -1,0 +1,265 @@
+from contextlib import ExitStack
+
+import concourse.mybir as mybir
+from concourse.masks import make_identity
+
+K, T, E, C, H, N = 2048, 640, 4, 128, 512, 128
+FLOPS = 2 * E * C * (2 * K * H + H * N)
+
+F32 = mybir.dt.float32
+BF16 = mybir.dt.bfloat16
+U32 = mybir.dt.uint32
+U16 = mybir.dt.uint16
+U8 = mybir.dt.uint8
+FP8X4 = mybir.dt.float8_e4m3fn_x4
+COPY = mybir.ActivationFunctionType.Copy
+RELU = mybir.ActivationFunctionType.Relu
+MULT = mybir.AluOpType.mult
+
+P = 128
+PACK = 4
+K_PASS = P * PACK
+PASSES = K // K_PASS
+
+X_VECTOR = 320
+W_VECTOR = 256
+GATHER = 256
+WARM_UP = 3
+
+
+def tile_moe_two_glu_relu_kernel(tc, xT, w1, w3, w2, gate, offs, dst, out):
+    nc = tc.nc
+    with ExitStack() as ctx:
+        keep = ctx.enter_context(tc.tile_pool(name="keep", bufs=1))
+        xraw = ctx.enter_context(tc.tile_pool(name="xraw", bufs=3))
+        xbf = ctx.enter_context(tc.tile_pool(name="xbf", bufs=2))
+        wraw = ctx.enter_context(tc.tile_pool(name="wraw", bufs=3))
+        wbf = ctx.enter_context(tc.tile_pool(name="wbf", bufs=4))
+        wq = ctx.enter_context(tc.tile_pool(name="wq", bufs=8))
+        hid = ctx.enter_context(tc.tile_pool(name="hid", bufs=2))
+        psum = ctx.enter_context(tc.psum_pool(name="psum", bufs=2))
+
+        offs_sb = keep.tile([P, E * C // 16], U16, name="offs_sb")
+        dst_sb = keep.tile([P, E * C // 16], U16, name="dst_sb")
+
+        ident = keep.tile([P, P], F32, name="ident")
+        make_identity(nc, ident[:])
+        out_sb = keep.tile([P, T], F32, name="out_sb")
+        nc.gpsimd.memset(out_sb[:], 0.0)
+
+        gate_sb = keep.tile([P, E * C], F32, name="gate_sb")
+        w2_first = keep.tile([P, 2, PACK * N], F32, name="w2_first")
+        w2_raw = {}
+        w2_bf = [keep.tile([P, 2, N, PACK], BF16, name=f"w2_bf{h}", align_bytes=64) for h in range(2)]
+        w2_codes = [keep.tile([P, 2 * N], U32, name=f"w2_codes{h}", align_bytes=64) for h in range(2)]
+        w2_scales = [keep.tile([P, 2 * N], U8, name=f"w2_scales{h}", align_bytes=64) for h in range(2)]
+
+        all_codes = [keep.tile([P, T], U32, name=f"all_codes{s}", align_bytes=64) for s in range(PASSES)]
+        all_scales = keep.tile([P, T], U8, name="all_scales", align_bytes=64)
+        slot_codes = [keep.tile([P, E * C], U32, name=f"slot_codes{s}", align_bytes=64) for s in range(PASSES)]
+        slot_scales = keep.tile([P, E * C], U8, name="slot_scales", align_bytes=64)
+        nc.gpsimd.memset(all_scales[:], 0)
+
+        def load_x(s):
+            raw = xraw.tile([P, PACK * T], F32, name="x_raw")
+            nc.sync.dma_start(raw[:], xT[s * K_PASS : (s + 1) * K_PASS, :].rearrange("(p j) t -> p (j t)", j=PACK))
+            return raw
+
+        def interleave_x(raw):
+            grouped = xbf.tile([P, T, PACK], BF16, name="x_grouped", align_bytes=64)
+            rows = raw[:].rearrange("p (j t) -> p t j", j=PACK)
+            nc.vector.tensor_copy(grouped[:, :X_VECTOR, :], rows[:, :X_VECTOR, :])
+            nc.scalar.activation(grouped[:, X_VECTOR:, :], rows[:, X_VECTOR:, :], COPY)
+            return grouped
+
+        def quantize_x(s, grouped):
+            flat = grouped[:].rearrange("p t j -> p (t j)")
+            for a, b in ((0, 512), (512, T)):
+                nc.vector.quantize_mx(
+                    out=all_codes[s][:, a:b].bitcast(FP8X4),
+                    scales=all_scales[4 * s :, a:b],
+                    in_=flat[:, a * PACK : b * PACK],
+                )
+
+        def gather_x(s, g):
+            cols = slice(g * GATHER, (g + 1) * GATHER)
+            idx = slice(g * GATHER // 16, (g + 1) * GATHER // 16)
+            nc.vector.tensor_copy(slot_codes[s][:, cols], all_codes[s][:].indirect(offs_sb[:, idx]))
+            if s == PASSES - 1:
+                nc.vector.tensor_copy(slot_scales[:, cols], all_scales[:].indirect(offs_sb[:, idx]))
+
+        def load_w(queue, raw, w, e, s0, s1):
+            rows = w[e, s0 * K_PASS : s1 * K_PASS, :]
+            queue.dma_start(raw[:, s0:s1, :], rows.rearrange("(s p j) i -> p s (j i)", p=P, j=PACK))
+
+        def load_w_rows(raw, w, e, s, j0, j1):
+            rows = w[e, s * K_PASS : (s + 1) * K_PASS, :].rearrange("(p j) i -> p j i", j=PACK)
+            cols = slice(j0 * H, j1 * H)
+            nc.sync.dma_start(
+                raw[:, s, cols].rearrange("p (j i) -> p j i", i=H), rows[:, j0:j1, :]
+            )
+
+        def interleave_w(raw, s, row_parts, vector_cols):
+            grouped = wbf.tile([P, H, PACK], BF16, name="w_grouped", align_bytes=64)
+            rows = raw[:, s, :].rearrange("p (j i) -> p i j", j=PACK)
+            for j0, j1 in row_parts:
+                m = vector_cols
+                nc.scalar.activation(grouped[:, m:, j0:j1], rows[:, m:, j0:j1], COPY)
+                nc.vector.tensor_copy(grouped[:, :m, j0:j1], rows[:, :m, j0:j1])
+            return grouped
+
+        def quantize_w(grouped):
+            codes = wq.tile([P, H], U32, name="w_codes", align_bytes=64)
+            scales = wq.tile([P, H], U8, name="w_scales", align_bytes=64)
+            nc.vector.quantize_mx(
+                out=codes[:].bitcast(FP8X4), scales=scales[:], in_=grouped[:].rearrange("p i j -> p (i j)")
+            )
+            return codes, scales
+
+        def multiply_w(acc, e, s, codes, scales, start, stop):
+            slots = slice(e * C, (e + 1) * C)
+            nc.tensor.matmul_mx(
+                out=acc[:],
+                lhsT=slot_codes[s][:, slots].bitcast(FP8X4),
+                lhsT_scale=slot_scales[4 * s :, slots],
+                rhs=codes[:].bitcast(FP8X4),
+                rhs_scale=scales[:],
+                start=start,
+                stop=stop,
+            )
+
+        def load_w2(h, raw):
+            w2_raw[h] = raw
+            nc.sync.dma_start(raw, w2[2 * h : 2 * h + 2].rearrange("e (p j) n -> p e (j n)", j=PACK))
+
+        def quantize_w2(h):
+            nc.scalar.activation(w2_bf[h][:], w2_raw[h].rearrange("p e (j n) -> p e n j", j=PACK), COPY)
+            nc.vector.quantize_mx(
+                out=w2_codes[h][:].bitcast(FP8X4),
+                scales=w2_scales[h][:],
+                in_=w2_bf[h][:].rearrange("p e n j -> p (e n j)"),
+            )
+
+        def hidden(a_acc_sb, b_acc):
+            h = hid.tile([P, H], BF16, name="h")
+            nc.vector.tensor_tensor(h[:], b_acc[:], a_acc_sb[:], MULT)
+            words = h[:].bitcast(F32)
+            turned = psum.tile([P, 2, P], F32, name="turned", bufs=1)
+            for u in range(2):
+                nc.tensor.transpose(turned[:, u, :], words[:, u : H // 2 : 2], ident[:])
+            grouped = hid.tile([P, C, PACK], BF16, name="h_grouped", align_bytes=64)
+            nc.scalar.copy(grouped[:].bitcast(F32), turned[:].rearrange("p u r -> p r u"))
+            return grouped
+
+        def quantize_h(grouped):
+            codes = hid.tile([P, C], U32, name="h_codes", align_bytes=64, bufs=E)
+            scales = hid.tile([P, C], U8, name="h_scales", align_bytes=64, bufs=E)
+            nc.vector.quantize_mx(
+                out=codes[:].bitcast(FP8X4), scales=scales[:], in_=grouped[:].rearrange("p c j -> p (c j)")
+            )
+            return codes, scales
+
+        def project(experts):
+            first, count = experts[0], len(experts)
+            y = psum.tile([N, count, C], F32, name=f"y{count}", bufs=3 - count)
+            for e in experts:
+                codes, scales = waiting[e]
+                cols = slice((e % 2) * N, (e % 2 + 1) * N)
+                nc.tensor.matmul_mx(
+                    out=y[:, e - first, :],
+                    lhsT=w2_codes[e // 2][:, cols].bitcast(FP8X4),
+                    lhsT_scale=w2_scales[e // 2][:, cols],
+                    rhs=codes[:].bitcast(FP8X4),
+                    rhs_scale=scales[:],
+                    start=True,
+                    stop=True,
+                )
+            y_sb = hid.tile([N, count * C], F32, name=f"y_sb{count}")
+            nc.scalar.copy(y_sb[:], y[:].rearrange("p e c -> p (e c)"))
+            return y_sb
+
+        def place(e, y):
+            idx = slice(e * C // 16, (e + 1) * C // 16)
+            nc.vector.tensor_tensor(out_sb[:].indirect(dst_sb[:, idx]), y, gate_sb[:, e * C : (e + 1) * C], MULT)
+
+        raws = [load_x(0)]
+        nc.sync.dma_start(offs_sb[:], offs)
+        raws += [load_x(s) for s in range(1, PASSES)]
+        nc.sync.dma_start(dst_sb[:], dst)
+        prev = None
+        for s in range(PASSES):
+            grouped = interleave_x(raws[s])
+            if prev is not None:
+                quantize_x(s - 1, prev)
+            prev = grouped
+            if s > 1:
+                gather_x(s - 2, 0)
+        quantize_x(PASSES - 1, prev)
+        gather_x(PASSES - 2, 0)
+        gather_x(PASSES - 1, 0)
+
+        chunks = [(m, e, s) for e in range(E) for m in range(2) for s in range(PASSES)]
+        last = len(chunks) - 1
+        acc = {}
+        relu_a = {}
+        waiting = {}
+        w_raw = {}
+        w_grouped = {}
+        for c in range(len(chunks) + 1):
+            if c <= last:
+                m, e, s = chunks[c]
+                w = (w1, w3)[m]
+                if s == 0:
+                    raw = wraw.tile([P, PASSES, PACK * H], F32, name="w_raw")
+                    w_raw[0] = raw
+                    if e == E - 1 and m == 1:
+                        load_w(nc.sync, raw, w, e, 0, 2)
+                        load_w(nc.sync, raw, w, e, 2, 3)
+                        load_w_rows(raw, w, e, 3, 0, 2)
+                        load_w_rows(raw, w, e, 3, 2, 4)
+                        tail = wraw.tile([P, PASSES, PACK * H], F32, name="w_raw")
+                        load_w2(1, tail[:, 0:2, : PACK * N])
+                    else:
+                        load_w(nc.sync, raw, w, e, 0, 2)
+                        load_w(nc.gpsimd, raw, w, e, 2, 4)
+                    if e == 0 and m == 1:
+                        load_w2(0, w2_first[:])
+                        nc.sync.dma_start(gate_sb[:], gate)
+                if c == last:
+                    w_grouped[c] = interleave_w(w_raw[0], s, ((0, 2), (2, 4)), 288)
+                else:
+                    w_grouped[c] = interleave_w(w_raw[0], s, ((0, 4),), W_VECTOR)
+            if c == 0:
+                continue
+            m, e, s = chunks[c - 1]
+            codes, scales = quantize_w(w_grouped.pop(c - 1))
+            if s == 0:
+                acc[m] = psum.tile([C, H], F32, name=("acc_a", "acc_b")[m])
+            multiply_w(acc[m], e, s, codes, scales, s == 0, s == PASSES - 1)
+            if c == last:
+                spare = psum.tile([C, H], F32, name="acc_a")
+                for repeat in range(WARM_UP):
+                    multiply_w(spare, e, s, codes, scales, True, True)
+            if m == 0 and s == PASSES - 1:
+                relu_a[e] = hid.tile([C, H], F32, name="relu_a")
+                nc.scalar.activation(relu_a[e][:], acc[0][:], RELU)
+            if e == 0 and m == 1:
+                gather_x(s, 1)
+            if m == 0 and s == 1 and e > 0:
+                if e == 1:
+                    quantize_w2(0)
+                waiting[e - 1] = quantize_h(waiting[e - 1])
+                if e == 2:
+                    y01 = project((0, 1))
+                    place(0, y01[:, :C])
+                    place(1, y01[:, C:])
+            if m == 1 and s == PASSES - 1:
+                waiting[e] = hidden(relu_a[e], acc[1])
+        waiting[3] = quantize_h(waiting[3])
+        quantize_w2(1)
+        y2 = project((2,))
+        y3 = project((3,))
+        place(2, y2[:])
+        place(3, y3[:])
+
+        nc.sync.dma_start(out, out_sb[:])

@@ -20,20 +20,22 @@ P = 128
 PACK = 4
 K_PASS = P * PACK
 PASSES = K // K_PASS
+HALF = H // 2
 
-X_VECTOR = 320
-W_VECTOR = 256
+X_VECTOR = 288
+W_VECTOR = 56
+W_VECTOR_END = 80
+END = 3
 GATHER = 256
-WARM_UP = 3
+RING = 12
 
 
 def tile_moe_two_glu_relu_kernel(tc, xT, w1, w3, w2, gate, offs, dst, out):
     nc = tc.nc
     with ExitStack() as ctx:
         keep = ctx.enter_context(tc.tile_pool(name="keep", bufs=1))
-        xraw = ctx.enter_context(tc.tile_pool(name="xraw", bufs=3))
+        ring = ctx.enter_context(tc.tile_pool(name="ring", bufs=RING))
         xbf = ctx.enter_context(tc.tile_pool(name="xbf", bufs=2))
-        wraw = ctx.enter_context(tc.tile_pool(name="wraw", bufs=3))
         wbf = ctx.enter_context(tc.tile_pool(name="wbf", bufs=4))
         wq = ctx.enter_context(tc.tile_pool(name="wq", bufs=8))
         hid = ctx.enter_context(tc.tile_pool(name="hid", bufs=2))
@@ -47,12 +49,9 @@ def tile_moe_two_glu_relu_kernel(tc, xT, w1, w3, w2, gate, offs, dst, out):
         out_sb = keep.tile([P, T], F32, name="out_sb")
         nc.gpsimd.memset(out_sb[:], 0.0)
 
+        gate_row = keep.tile([P, PACK], F32, name="gate_row")
         gate_sb = keep.tile([P, E * C], F32, name="gate_sb")
-        w2_first = keep.tile([P, 2, PACK * N], F32, name="w2_first")
-        w2_raw = {}
-        w2_bf = [keep.tile([P, 2, N, PACK], BF16, name=f"w2_bf{h}", align_bytes=64) for h in range(2)]
-        w2_codes = [keep.tile([P, 2 * N], U32, name=f"w2_codes{h}", align_bytes=64) for h in range(2)]
-        w2_scales = [keep.tile([P, 2 * N], U8, name=f"w2_scales{h}", align_bytes=64) for h in range(2)]
+        w2_codes = {}
 
         all_codes = [keep.tile([P, T], U32, name=f"all_codes{s}", align_bytes=64) for s in range(PASSES)]
         all_scales = keep.tile([P, T], U8, name="all_scales", align_bytes=64)
@@ -60,14 +59,22 @@ def tile_moe_two_glu_relu_kernel(tc, xT, w1, w3, w2, gate, offs, dst, out):
         slot_scales = keep.tile([P, E * C], U8, name="slot_scales", align_bytes=64)
         nc.gpsimd.memset(all_scales[:], 0)
 
-        def load_x(s):
-            raw = xraw.tile([P, PACK * T], F32, name="x_raw")
-            nc.sync.dma_start(raw[:], xT[s * K_PASS : (s + 1) * K_PASS, :].rearrange("(p j) t -> p (j t)", j=PACK))
+        def load_rows(matrix, s, j0, j1):
+            width = matrix.shape[1]
+            raw = ring.tile([P, j1 - j0, width], F32, name="raw")
+            rows = matrix[s * K_PASS : (s + 1) * K_PASS, :].rearrange("(p j) i -> p j i", j=PACK)
+            nc.sync.dma_start(raw[:], rows[:, j0:j1, :])
             return raw
+
+        def spread_gate():
+            bank = psum.tile([P, PACK, P], F32, name="turned", bufs=1)
+            for m in range(PACK):
+                nc.tensor.transpose(bank[:, m, :], gate_row[:, m : m + 1].to_broadcast([P, P]), ident[:])
+            nc.scalar.copy(gate_sb[:].rearrange("p (n m) -> p n m", m=PACK), bank[:].rearrange("p m n -> p n m"))
 
         def interleave_x(raw):
             grouped = xbf.tile([P, T, PACK], BF16, name="x_grouped", align_bytes=64)
-            rows = raw[:].rearrange("p (j t) -> p t j", j=PACK)
+            rows = raw[:].rearrange("p j t -> p t j")
             nc.vector.tensor_copy(grouped[:, :X_VECTOR, :], rows[:, :X_VECTOR, :])
             nc.scalar.activation(grouped[:, X_VECTOR:, :], rows[:, X_VECTOR:, :], COPY)
             return grouped
@@ -88,178 +95,145 @@ def tile_moe_two_glu_relu_kernel(tc, xT, w1, w3, w2, gate, offs, dst, out):
             if s == PASSES - 1:
                 nc.vector.tensor_copy(slot_scales[:, cols], all_scales[:].indirect(offs_sb[:, idx]))
 
-        def load_w(queue, raw, w, e, s0, s1):
-            rows = w[e, s0 * K_PASS : s1 * K_PASS, :]
-            queue.dma_start(raw[:, s0:s1, :], rows.rearrange("(s p j) i -> p s (j i)", p=P, j=PACK))
+        def interleave_w(grouped, raw, j0, j1, share):
+            rows = raw[:].rearrange("p j (q u e) -> p q u e j", u=2, e=2)
+            into = grouped[:].rearrange("p u q e j -> p q u e j")[:, :, :, :, j0:j1]
+            nc.scalar.copy(into[:, share:], rows[:, share:])
+            nc.vector.tensor_copy(into[:, :share], rows[:, :share])
 
-        def load_w_rows(raw, w, e, s, j0, j1):
-            rows = w[e, s * K_PASS : (s + 1) * K_PASS, :].rearrange("(p j) i -> p j i", j=PACK)
-            cols = slice(j0 * H, j1 * H)
-            nc.sync.dma_start(
-                raw[:, s, cols].rearrange("p (j i) -> p j i", i=H), rows[:, j0:j1, :]
-            )
-
-        def interleave_w(raw, s, row_parts, vector_cols):
-            grouped = wbf.tile([P, H, PACK], BF16, name="w_grouped", align_bytes=64)
-            rows = raw[:, s, :].rearrange("p (j i) -> p i j", j=PACK)
-            for j0, j1 in row_parts:
-                m = vector_cols
-                nc.scalar.activation(grouped[:, m:, j0:j1], rows[:, m:, j0:j1], COPY)
-                nc.vector.tensor_copy(grouped[:, :m, j0:j1], rows[:, :m, j0:j1])
-            return grouped
-
-        def quantize_w(grouped):
-            codes = wq.tile([P, H], U32, name="w_codes", align_bytes=64)
-            scales = wq.tile([P, H], U8, name="w_scales", align_bytes=64)
-            nc.vector.quantize_mx(
-                out=codes[:].bitcast(FP8X4), scales=scales[:], in_=grouped[:].rearrange("p i j -> p (i j)")
-            )
+        def quantize(values, name, pool, bufs):
+            width = values.shape[1] // PACK
+            codes = pool.tile([P, width], U32, name=name + "_codes", align_bytes=64, bufs=bufs)
+            scales = pool.tile([P, width], U8, name=name + "_scales", align_bytes=64, bufs=bufs)
+            nc.vector.quantize_mx(out=codes[:].bitcast(FP8X4), scales=scales[:], in_=values)
             return codes, scales
 
-        def multiply_w(acc, e, s, codes, scales, start, stop):
+        def multiply_w(acc, e, s, codes, scales):
             slots = slice(e * C, (e + 1) * C)
             nc.tensor.matmul_mx(
-                out=acc[:],
+                out=acc,
                 lhsT=slot_codes[s][:, slots].bitcast(FP8X4),
                 lhsT_scale=slot_scales[4 * s :, slots],
-                rhs=codes[:].bitcast(FP8X4),
-                rhs_scale=scales[:],
-                start=start,
-                stop=stop,
+                rhs=codes.bitcast(FP8X4),
+                rhs_scale=scales,
+                start=s == 0,
+                stop=s == PASSES - 1,
             )
 
-        def load_w2(h, raw):
-            w2_raw[h] = raw
-            nc.sync.dma_start(raw, w2[2 * h : 2 * h + 2].rearrange("e (p j) n -> p e (j n)", j=PACK))
+        def quantize_w2(e, raw):
+            grouped = hid.tile([P, N, PACK], BF16, name="w2_grouped", align_bytes=64)
+            nc.scalar.activation(grouped[:], raw[:].rearrange("p j n -> p n j"), COPY)
+            w2_codes[e] = quantize(grouped[:].rearrange("p n j -> p (n j)"), "w2", hid, E)
 
-        def quantize_w2(h):
-            nc.scalar.activation(w2_bf[h][:], w2_raw[h].rearrange("p e (j n) -> p e n j", j=PACK), COPY)
-            nc.vector.quantize_mx(
-                out=w2_codes[h][:].bitcast(FP8X4),
-                scales=w2_scales[h][:],
-                in_=w2_bf[h][:].rearrange("p e n j -> p (e n j)"),
-            )
-
-        def hidden(a_acc_sb, b_acc):
+        def hidden(a_sb, b_acc):
             h = hid.tile([P, H], BF16, name="h")
-            nc.vector.tensor_tensor(h[:], b_acc[:], a_acc_sb[:], MULT)
             words = h[:].bitcast(F32)
             turned = psum.tile([P, 2, P], F32, name="turned", bufs=1)
             for u in range(2):
-                nc.tensor.transpose(turned[:, u, :], words[:, u : H // 2 : 2], ident[:])
+                cols = slice(u * HALF, (u + 1) * HALF)
+                nc.vector.tensor_tensor(h[:, cols], b_acc[u][:], a_sb[:, cols], MULT)
+                nc.tensor.transpose(turned[:, u, :], words[:, u * P : (u + 1) * P], ident[:])
             grouped = hid.tile([P, C, PACK], BF16, name="h_grouped", align_bytes=64)
             nc.scalar.copy(grouped[:].bitcast(F32), turned[:].rearrange("p u r -> p r u"))
             return grouped
 
-        def quantize_h(grouped):
-            codes = hid.tile([P, C], U32, name="h_codes", align_bytes=64, bufs=E)
-            scales = hid.tile([P, C], U8, name="h_scales", align_bytes=64, bufs=E)
-            nc.vector.quantize_mx(
-                out=codes[:].bitcast(FP8X4), scales=scales[:], in_=grouped[:].rearrange("p c j -> p (c j)")
+        def project(e, h_codes):
+            y = psum.tile([N, C], F32, name="y")
+            nc.tensor.matmul_mx(
+                out=y[:],
+                lhsT=w2_codes[e][0][:].bitcast(FP8X4),
+                lhsT_scale=w2_codes[e][1][:],
+                rhs=h_codes[0][:].bitcast(FP8X4),
+                rhs_scale=h_codes[1][:],
+                start=True,
+                stop=True,
             )
-            return codes, scales
-
-        def project(experts):
-            first, count = experts[0], len(experts)
-            y = psum.tile([N, count, C], F32, name=f"y{count}", bufs=3 - count)
-            for e in experts:
-                codes, scales = waiting[e]
-                cols = slice((e % 2) * N, (e % 2 + 1) * N)
-                nc.tensor.matmul_mx(
-                    out=y[:, e - first, :],
-                    lhsT=w2_codes[e // 2][:, cols].bitcast(FP8X4),
-                    lhsT_scale=w2_scales[e // 2][:, cols],
-                    rhs=codes[:].bitcast(FP8X4),
-                    rhs_scale=scales[:],
-                    start=True,
-                    stop=True,
-                )
-            y_sb = hid.tile([N, count * C], F32, name=f"y_sb{count}")
-            nc.scalar.copy(y_sb[:], y[:].rearrange("p e c -> p (e c)"))
-            return y_sb
-
-        def place(e, y):
+            y_sb = hid.tile([N, C], F32, name="y_sb")
+            nc.scalar.copy(y_sb[:], y[:])
             idx = slice(e * C // 16, (e + 1) * C // 16)
-            nc.vector.tensor_tensor(out_sb[:].indirect(dst_sb[:, idx]), y, gate_sb[:, e * C : (e + 1) * C], MULT)
+            nc.vector.tensor_tensor(
+                out_sb[:].indirect(dst_sb[:, idx]), y_sb[:], gate_sb[:, e * C : (e + 1) * C], MULT
+            )
 
-        raws = [load_x(0)]
+        raws = [load_rows(xT, 0, 0, PACK)]
         nc.sync.dma_start(offs_sb[:], offs)
-        raws += [load_x(s) for s in range(1, PASSES)]
+        raws += [load_rows(xT, s, 0, PACK) for s in range(1, PASSES)]
         nc.sync.dma_start(dst_sb[:], dst)
+        nc.sync.dma_start(gate_row[:], gate[0:1, :].rearrange("o (n m) -> (o n) m", m=PACK))
         prev = None
         for s in range(PASSES):
-            grouped = interleave_x(raws[s])
             if prev is not None:
                 quantize_x(s - 1, prev)
-            prev = grouped
-            if s > 1:
-                gather_x(s - 2, 0)
+            prev = interleave_x(raws[s])
+            if s > 0:
+                gather_x(s - 1, 0)
         quantize_x(PASSES - 1, prev)
-        gather_x(PASSES - 2, 0)
         gather_x(PASSES - 1, 0)
+        spread_gate()
 
         chunks = [(m, e, s) for e in range(E) for m in range(2) for s in range(PASSES)]
         last = len(chunks) - 1
-        acc = {}
+        acc_a = {}
+        acc_b = {}
         relu_a = {}
-        waiting = {}
-        w_raw = {}
+        h_grouped = {}
+        h_codes = {}
+        w2_raw = {}
         w_grouped = {}
-        for c in range(len(chunks) + 1):
-            if c <= last:
-                m, e, s = chunks[c]
-                w = (w1, w3)[m]
+
+        def finish_chunk(c):
+            m, e, s = chunks[c]
+            flat = w_grouped.pop(c)[:].rearrange("p u q e j -> p (u q e j)")
+            if m == 0:
+                codes, scales = quantize(flat, "w", wq, 8)
                 if s == 0:
-                    raw = wraw.tile([P, PASSES, PACK * H], F32, name="w_raw")
-                    w_raw[0] = raw
-                    if e == E - 1 and m == 1:
-                        load_w(nc.sync, raw, w, e, 0, 2)
-                        load_w(nc.sync, raw, w, e, 2, 3)
-                        load_w_rows(raw, w, e, 3, 0, 2)
-                        load_w_rows(raw, w, e, 3, 2, 4)
-                        tail = wraw.tile([P, PASSES, PACK * H], F32, name="w_raw")
-                        load_w2(1, tail[:, 0:2, : PACK * N])
-                    else:
-                        load_w(nc.sync, raw, w, e, 0, 2)
-                        load_w(nc.gpsimd, raw, w, e, 2, 4)
-                    if e == 0 and m == 1:
-                        load_w2(0, w2_first[:])
-                        nc.sync.dma_start(gate_sb[:], gate)
+                    acc_a[e] = psum.tile([C, H], F32, name="acc_a")
+                multiply_w(acc_a[e][:], e, s, codes[:], scales[:])
+                if s == PASSES - 1:
+                    relu_a[e] = hid.tile([C, H], F32, name="relu_a")
+                    nc.scalar.activation(relu_a[e][:], acc_a[e][:], RELU)
+            else:
+                if s == 0:
+                    acc_b[e] = [psum.tile([C, HALF], F32, name="acc_b") for u in range(2)]
                 if c == last:
-                    w_grouped[c] = interleave_w(w_raw[0], s, ((0, 2), (2, 4)), 288)
+                    for u in range(2):
+                        codes, scales = quantize(flat[:, u * HALF * PACK : (u + 1) * HALF * PACK], "w", wq, 8)
+                        multiply_w(acc_b[e][u][:], e, s, codes[:], scales[:])
                 else:
-                    w_grouped[c] = interleave_w(w_raw[0], s, ((0, 4),), W_VECTOR)
-            if c == 0:
-                continue
-            m, e, s = chunks[c - 1]
-            codes, scales = quantize_w(w_grouped.pop(c - 1))
-            if s == 0:
-                acc[m] = psum.tile([C, H], F32, name=("acc_a", "acc_b")[m])
-            multiply_w(acc[m], e, s, codes, scales, s == 0, s == PASSES - 1)
-            if c == last:
-                spare = psum.tile([C, H], F32, name="acc_a")
-                for repeat in range(WARM_UP):
-                    multiply_w(spare, e, s, codes, scales, True, True)
-            if m == 0 and s == PASSES - 1:
-                relu_a[e] = hid.tile([C, H], F32, name="relu_a")
-                nc.scalar.activation(relu_a[e][:], acc[0][:], RELU)
+                    codes, scales = quantize(flat, "w", wq, 8)
+                    for u in range(2):
+                        cols = slice(u * HALF, (u + 1) * HALF)
+                        multiply_w(acc_b[e][u][:], e, s, codes[:, cols], scales[:, cols])
+                if s == PASSES - 1:
+                    h_grouped[e] = hidden(relu_a[e], acc_b[e])
             if e == 0 and m == 1:
                 gather_x(s, 1)
             if m == 0 and s == 1 and e > 0:
-                if e == 1:
-                    quantize_w2(0)
-                waiting[e - 1] = quantize_h(waiting[e - 1])
-                if e == 2:
-                    y01 = project((0, 1))
-                    place(0, y01[:, :C])
-                    place(1, y01[:, C:])
-            if m == 1 and s == PASSES - 1:
-                waiting[e] = hidden(relu_a[e], acc[1])
-        waiting[3] = quantize_h(waiting[3])
-        quantize_w2(1)
-        y2 = project((2,))
-        y3 = project((3,))
-        place(2, y2[:])
-        place(3, y3[:])
+                h_codes[e - 1] = quantize(h_grouped[e - 1][:].rearrange("p c j -> p (c j)"), "h", hid, E)
+                if e - 1 < 2:
+                    quantize_w2(e - 1, w2_raw[e - 1])
+                    project(e - 1, h_codes[e - 1])
+
+        for c in range(len(chunks)):
+            m, e, s = chunks[c]
+            w = (w1, w3)[m]
+            parts = ((0, 2), (2, PACK)) if c == last else ((0, PACK),)
+            raw_parts = [load_rows(w[e], s, j0, j1) for j0, j1 in parts]
+            if m == 1 and s == PASSES - 1 and e < 2:
+                w2_raw[e] = load_rows(w2[e], 0, 0, PACK)
+            if c == last:
+                for late in (2, 3):
+                    w2_raw[late] = load_rows(w2[late], 0, 0, PACK)
+            if c > 0:
+                finish_chunk(c - 1)
+            w_grouped[c] = wbf.tile([P, 2, P, 2, PACK], BF16, name="w_grouped", align_bytes=64)
+            for raw, (j0, j1) in zip(raw_parts, parts):
+                interleave_w(w_grouped[c], raw, j0, j1, W_VECTOR_END if c > last - END else W_VECTOR)
+        quantize_w2(2, w2_raw[2])
+        finish_chunk(last)
+        quantize_w2(3, w2_raw[3])
+        h_codes[3] = quantize(h_grouped[3][:].rearrange("p c j -> p (c j)"), "h", hid, E)
+        project(2, h_codes[2])
+        project(3, h_codes[3])
 
         nc.sync.dma_start(out, out_sb[:])

@@ -27,14 +27,15 @@ W_VECTOR = 56
 W_VECTOR_END = 80
 END = 3
 GATHER = 256
-RING = 12
+ARENA = 144 * 1024
+PASSES_A_LOAD = (4, 4, 2, 1)
 
 
 def tile_moe_two_glu_relu_kernel(tc, xT, w1, w3, w2, gate, offs, dst, out):
     nc = tc.nc
     with ExitStack() as ctx:
         keep = ctx.enter_context(tc.tile_pool(name="keep", bufs=1))
-        ring = ctx.enter_context(tc.tile_pool(name="ring", bufs=RING))
+        ring = ctx.enter_context(tc.tile_pool(name="ring", bufs=1))
         xbf = ctx.enter_context(tc.tile_pool(name="xbf", bufs=2))
         wbf = ctx.enter_context(tc.tile_pool(name="wbf", bufs=4))
         wq = ctx.enter_context(tc.tile_pool(name="wq", bufs=8))
@@ -59,12 +60,26 @@ def tile_moe_two_glu_relu_kernel(tc, xT, w1, w3, w2, gate, offs, dst, out):
         slot_scales = keep.tile([P, E * C], U8, name="slot_scales", align_bytes=64)
         nc.gpsimd.memset(all_scales[:], 0)
 
+        placed = [0]
+
+        def ring_tile(shape):
+            size = 4 * shape[1] * shape[2]
+            start = placed[-1] if placed[-1] + size <= ARENA else 0
+            placed.append(start + size)
+            return ring.tile(shape, F32, name=f"raw{len(placed)}", offset=start)
+
         def load_rows(matrix, s, j0, j1):
-            width = matrix.shape[1]
-            raw = ring.tile([P, j1 - j0, width], F32, name="raw")
+            raw = ring_tile([P, j1 - j0, matrix.shape[1]])
             rows = matrix[s * K_PASS : (s + 1) * K_PASS, :].rearrange("(p j) i -> p j i", j=PACK)
             nc.sync.dma_start(raw[:], rows[:, j0:j1, :])
-            return raw
+            return raw[:]
+
+        def load_passes(matrix, s0, count):
+            width = matrix.shape[1]
+            raw = ring_tile([P, count, PACK * width])
+            rows = matrix[s0 * K_PASS : (s0 + count) * K_PASS, :]
+            nc.sync.dma_start(raw[:], rows.rearrange("(s p j) i -> p s (j i)", p=P, j=PACK))
+            return [raw[:, s, :].rearrange("p (j i) -> p j i", j=PACK) for s in range(count)]
 
         def spread_gate():
             bank = psum.tile([P, PACK, P], F32, name="turned", bufs=1)
@@ -74,7 +89,7 @@ def tile_moe_two_glu_relu_kernel(tc, xT, w1, w3, w2, gate, offs, dst, out):
 
         def interleave_x(raw):
             grouped = xbf.tile([P, T, PACK], BF16, name="x_grouped", align_bytes=64)
-            rows = raw[:].rearrange("p j t -> p t j")
+            rows = raw.rearrange("p j t -> p t j")
             nc.vector.tensor_copy(grouped[:, :X_VECTOR, :], rows[:, :X_VECTOR, :])
             nc.scalar.activation(grouped[:, X_VECTOR:, :], rows[:, X_VECTOR:, :], COPY)
             return grouped
@@ -96,8 +111,8 @@ def tile_moe_two_glu_relu_kernel(tc, xT, w1, w3, w2, gate, offs, dst, out):
                 nc.vector.tensor_copy(slot_scales[:, cols], all_scales[:].indirect(offs_sb[:, idx]))
 
         def interleave_w(grouped, raw, j0, j1, share):
-            rows = raw[:].rearrange("p j (q u e) -> p q u e j", u=2, e=2)
-            into = grouped[:].rearrange("p u q e j -> p q u e j")[:, :, :, :, j0:j1]
+            rows = raw.rearrange("p j (q u e) -> p q j u e", u=2, e=2)
+            into = grouped[:].rearrange("p u q e j -> p q j u e")[:, :, j0:j1]
             nc.scalar.copy(into[:, share:], rows[:, share:])
             nc.vector.tensor_copy(into[:, :share], rows[:, :share])
 
@@ -122,7 +137,7 @@ def tile_moe_two_glu_relu_kernel(tc, xT, w1, w3, w2, gate, offs, dst, out):
 
         def quantize_w2(e, raw):
             grouped = hid.tile([P, N, PACK], BF16, name="w2_grouped", align_bytes=64)
-            nc.scalar.activation(grouped[:], raw[:].rearrange("p j n -> p n j"), COPY)
+            nc.scalar.activation(grouped[:], raw.rearrange("p j n -> p n j"), COPY)
             w2_codes[e] = quantize(grouped[:].rearrange("p n j -> p (n j)"), "w2", hid, E)
 
         def hidden(a_sb, b_acc):
@@ -155,9 +170,9 @@ def tile_moe_two_glu_relu_kernel(tc, xT, w1, w3, w2, gate, offs, dst, out):
                 out_sb[:].indirect(dst_sb[:, idx]), y_sb[:], gate_sb[:, e * C : (e + 1) * C], MULT
             )
 
-        raws = [load_rows(xT, 0, 0, PACK)]
+        raws = load_passes(xT, 0, 2)
         nc.sync.dma_start(offs_sb[:], offs)
-        raws += [load_rows(xT, s, 0, PACK) for s in range(1, PASSES)]
+        raws += load_passes(xT, 2, 2)
         nc.sync.dma_start(dst_sb[:], dst)
         nc.sync.dma_start(gate_row[:], gate[0:1, :].rearrange("o (n m) -> (o n) m", m=PACK))
         prev = None
@@ -218,9 +233,15 @@ def tile_moe_two_glu_relu_kernel(tc, xT, w1, w3, w2, gate, offs, dst, out):
             m, e, s = chunks[c]
             w = (w1, w3)[m]
             parts = ((0, 2), (2, PACK)) if c == last else ((0, PACK),)
-            raw_parts = [load_rows(w[e], s, j0, j1) for j0, j1 in parts]
-            if m == 1 and s == PASSES - 1 and e < 2:
-                w2_raw[e] = load_rows(w2[e], 0, 0, PACK)
+            count = PASSES_A_LOAD[e]
+            if c == last:
+                raw_parts = [load_rows(w[e], s, j0, j1) for j0, j1 in parts]
+            else:
+                if s % count == 0:
+                    loaded = load_passes(w[e], s, count)
+                raw_parts = [loaded[s % count]]
+            if m == 1 and s == PASSES - 1 and e == 0:
+                w2_raw[0], w2_raw[1] = load_passes(w2[0:2].rearrange("e i n -> (e i) n"), 0, 2)
             if c == last:
                 for late in (2, 3):
                     w2_raw[late] = load_rows(w2[late], 0, 0, PACK)

@@ -26,6 +26,7 @@ X_VECTOR = 288
 W_VECTOR = 56
 W_VECTOR_END = 80
 END = 3
+LAST_VECTOR = 40
 GATHER = 256
 ARENA = 144 * 1024
 PASSES_A_LOAD = (4, 4, 2, 1)
@@ -116,6 +117,13 @@ def tile_moe_two_glu_relu_kernel(tc, xT, w1, w3, w2, gate, offs, dst, out):
             nc.scalar.copy(into[:, share:], rows[:, share:])
             nc.vector.tensor_copy(into[:, :share], rows[:, :share])
 
+        def interleave_last(grouped, raw, j0, j1):
+            rows = raw.rearrange("p j (q u e) -> p u q j e", u=2, e=2)
+            into = grouped[:].rearrange("p u q e j -> p u q j e")[:, :, :, j0:j1]
+            nc.scalar.copy(into[:, 1, LAST_VECTOR:], rows[:, 1, LAST_VECTOR:])
+            nc.vector.tensor_copy(into[:, 0], rows[:, 0])
+            nc.vector.tensor_copy(into[:, 1, :LAST_VECTOR], rows[:, 1, :LAST_VECTOR])
+
         def quantize(values, name, pool, bufs):
             width = values.shape[1] // PACK
             codes = pool.tile([P, width], U32, name=name + "_codes", align_bytes=64, bufs=bufs)
@@ -123,7 +131,7 @@ def tile_moe_two_glu_relu_kernel(tc, xT, w1, w3, w2, gate, offs, dst, out):
             nc.vector.quantize_mx(out=codes[:].bitcast(FP8X4), scales=scales[:], in_=values)
             return codes, scales
 
-        def multiply_w(acc, e, s, codes, scales):
+        def multiply_w(acc, e, s, codes, scales, alone=False):
             slots = slice(e * C, (e + 1) * C)
             nc.tensor.matmul_mx(
                 out=acc,
@@ -131,17 +139,20 @@ def tile_moe_two_glu_relu_kernel(tc, xT, w1, w3, w2, gate, offs, dst, out):
                 lhsT_scale=slot_scales[4 * s :, slots],
                 rhs=codes.bitcast(FP8X4),
                 rhs_scale=scales,
-                start=s == 0,
-                stop=s == PASSES - 1,
+                start=alone or s == 0,
+                stop=alone or s == PASSES - 1,
             )
 
         def quantize_w2(e, raw):
-            grouped = hid.tile([P, N, PACK], BF16, name="w2_grouped", align_bytes=64)
-            nc.scalar.activation(grouped[:], raw.rearrange("p j n -> p n j"), COPY)
+            tag = "h" if e == E - 2 else "w2_grouped"
+            grouped = hid.tile([P, N, PACK], BF16, name=tag, align_bytes=64, bufs=1)
+            nc.scalar.copy(
+                grouped[:].rearrange("p (q i) j -> p q j i", i=PACK), raw.rearrange("p j (q i) -> p q j i", i=PACK)
+            )
             w2_codes[e] = quantize(grouped[:].rearrange("p n j -> p (n j)"), "w2", hid, E)
 
         def hidden(a_sb, b_acc):
-            h = hid.tile([P, H], BF16, name="h")
+            h = hid.tile([P, H], BF16, name="h", align_bytes=64, bufs=1)
             words = h[:].bitcast(F32)
             turned = psum.tile([P, 2, P], F32, name="turned", bufs=1)
             for u in range(2):
@@ -165,6 +176,9 @@ def tile_moe_two_glu_relu_kernel(tc, xT, w1, w3, w2, gate, offs, dst, out):
             )
             y_sb = hid.tile([N, C], F32, name="y_sb")
             nc.scalar.copy(y_sb[:], y[:])
+            return y_sb
+
+        def place(e, y_sb):
             idx = slice(e * C // 16, (e + 1) * C // 16)
             nc.vector.tensor_tensor(
                 out_sb[:].indirect(dst_sb[:, idx]), y_sb[:], gate_sb[:, e * C : (e + 1) * C], MULT
@@ -189,6 +203,8 @@ def tile_moe_two_glu_relu_kernel(tc, xT, w1, w3, w2, gate, offs, dst, out):
         chunks = [(m, e, s) for e in range(E) for m in range(2) for s in range(PASSES)]
         last = len(chunks) - 1
         acc_a = {}
+        warm = []
+        y_late = []
         acc_b = {}
         relu_a = {}
         h_grouped = {}
@@ -214,11 +230,17 @@ def tile_moe_two_glu_relu_kernel(tc, xT, w1, w3, w2, gate, offs, dst, out):
                     for u in range(2):
                         codes, scales = quantize(flat[:, u * HALF * PACK : (u + 1) * HALF * PACK], "w", wq, 8)
                         multiply_w(acc_b[e][u][:], e, s, codes[:], scales[:])
+                    quantize_w2(2, w2_raw[2])
+                    y_late.append(project(2, h_codes[2]))
                 else:
                     codes, scales = quantize(flat, "w", wq, 8)
                     for u in range(2):
                         cols = slice(u * HALF, (u + 1) * HALF)
                         multiply_w(acc_b[e][u][:], e, s, codes[:, cols], scales[:, cols])
+                    if c == last - 1 or c == last - 2:
+                        warm.append((codes, scales))
+                        spare = psum.tile([C, H], F32, name="acc_a")
+                        multiply_w(spare[:], e, s, codes[:], scales[:], True)
                 if s == PASSES - 1:
                     h_grouped[e] = hidden(relu_a[e], acc_b[e])
             if e == 0 and m == 1:
@@ -227,7 +249,7 @@ def tile_moe_two_glu_relu_kernel(tc, xT, w1, w3, w2, gate, offs, dst, out):
                 h_codes[e - 1] = quantize(h_grouped[e - 1][:].rearrange("p c j -> p (c j)"), "h", hid, E)
                 if e - 1 < 2:
                     quantize_w2(e - 1, w2_raw[e - 1])
-                    project(e - 1, h_codes[e - 1])
+                    place(e - 1, project(e - 1, h_codes[e - 1]))
 
         for c in range(len(chunks)):
             m, e, s = chunks[c]
@@ -249,12 +271,17 @@ def tile_moe_two_glu_relu_kernel(tc, xT, w1, w3, w2, gate, offs, dst, out):
                 finish_chunk(c - 1)
             w_grouped[c] = wbf.tile([P, 2, P, 2, PACK], BF16, name="w_grouped", align_bytes=64)
             for raw, (j0, j1) in zip(raw_parts, parts):
-                interleave_w(w_grouped[c], raw, j0, j1, W_VECTOR_END if c > last - END else W_VECTOR)
-        quantize_w2(2, w2_raw[2])
+                if j0 > 0:
+                    interleave_last(w_grouped[c], raw, j0, j1)
+                else:
+                    interleave_w(w_grouped[c], raw, j0, j1, W_VECTOR_END if c > last - END else W_VECTOR)
         finish_chunk(last)
+        for u in range(2):
+            spare = psum.tile([C, H], F32, name="acc_b")
+            multiply_w(spare[:], E - 1, 2, warm[1][0][:], warm[1][1][:], True)
+        place(2, y_late[0])
         quantize_w2(3, w2_raw[3])
         h_codes[3] = quantize(h_grouped[3][:].rearrange("p c j -> p (c j)"), "h", hid, E)
-        project(2, h_codes[2])
-        project(3, h_codes[3])
+        place(3, project(3, h_codes[3]))
 
         nc.sync.dma_start(out, out_sb[:])

@@ -131,7 +131,7 @@ def tile_moe_two_glu_relu_kernel(tc, xT, w1, w3, w2, gate, offs, dst, out):
             nc.vector.quantize_mx(out=codes[:].bitcast(FP8X4), scales=scales[:], in_=values)
             return codes, scales
 
-        def multiply_w(acc, e, s, codes, scales, alone=False):
+        def multiply_w(acc, e, s, codes, scales):
             slots = slice(e * C, (e + 1) * C)
             nc.tensor.matmul_mx(
                 out=acc,
@@ -139,8 +139,8 @@ def tile_moe_two_glu_relu_kernel(tc, xT, w1, w3, w2, gate, offs, dst, out):
                 lhsT_scale=slot_scales[4 * s :, slots],
                 rhs=codes.bitcast(FP8X4),
                 rhs_scale=scales,
-                start=alone or s == 0,
-                stop=alone or s == PASSES - 1,
+                start=s == 0,
+                stop=s == PASSES - 1,
             )
 
         def quantize_w2(e, raw):
@@ -203,7 +203,6 @@ def tile_moe_two_glu_relu_kernel(tc, xT, w1, w3, w2, gate, offs, dst, out):
         chunks = [(m, e, s) for e in range(E) for m in range(2) for s in range(PASSES)]
         last = len(chunks) - 1
         acc_a = {}
-        warm = []
         y_late = []
         acc_b = {}
         relu_a = {}
@@ -237,10 +236,6 @@ def tile_moe_two_glu_relu_kernel(tc, xT, w1, w3, w2, gate, offs, dst, out):
                     for u in range(2):
                         cols = slice(u * HALF, (u + 1) * HALF)
                         multiply_w(acc_b[e][u][:], e, s, codes[:, cols], scales[:, cols])
-                    if c == last - 1 or c == last - 2:
-                        warm.append((codes, scales))
-                        spare = psum.tile([C, H], F32, name="acc_a")
-                        multiply_w(spare[:], e, s, codes[:], scales[:], True)
                 if s == PASSES - 1:
                     h_grouped[e] = hidden(relu_a[e], acc_b[e])
             if e == 0 and m == 1:
@@ -276,9 +271,6 @@ def tile_moe_two_glu_relu_kernel(tc, xT, w1, w3, w2, gate, offs, dst, out):
                 else:
                     interleave_w(w_grouped[c], raw, j0, j1, W_VECTOR_END if c > last - END else W_VECTOR)
         finish_chunk(last)
-        for u in range(2):
-            spare = psum.tile([C, H], F32, name="acc_b")
-            multiply_w(spare[:], E - 1, 2, warm[1][0][:], warm[1][1][:], True)
         place(2, y_late[0])
         quantize_w2(3, w2_raw[3])
         h_codes[3] = quantize(h_grouped[3][:].rearrange("p c j -> p (c j)"), "h", hid, E)

@@ -22,14 +22,14 @@ K_PASS = P * PACK
 PASSES = K // K_PASS
 HALF = H // 2
 
-X_VECTOR = 288
-W_VECTOR = 56
-W_VECTOR_END = 80
+X_VECTOR = 208
+W_VECTOR = 50
+W_VECTOR_END = 72
 END = 3
 LAST_VECTOR = 40
 GATHER = 256
 ARENA = 144 * 1024
-PASSES_A_LOAD = (4, 4, 2, 1)
+PASSES_A_LOAD = (2, 2, 2, 1)
 
 
 def tile_moe_two_glu_relu_kernel(tc, xT, w1, w3, w2, gate, offs, dst, out):
@@ -90,9 +90,11 @@ def tile_moe_two_glu_relu_kernel(tc, xT, w1, w3, w2, gate, offs, dst, out):
 
         def interleave_x(raw):
             grouped = xbf.tile([P, T, PACK], BF16, name="x_grouped", align_bytes=64)
-            rows = raw.rearrange("p j t -> p t j")
-            nc.vector.tensor_copy(grouped[:, :X_VECTOR, :], rows[:, :X_VECTOR, :])
-            nc.scalar.activation(grouped[:, X_VECTOR:, :], rows[:, X_VECTOR:, :], COPY)
+            rows = raw.rearrange("p j (q i) -> p q j i", i=PACK)
+            into = grouped[:].rearrange("p (q i) j -> p q j i", i=PACK)
+            share = X_VECTOR // PACK
+            nc.vector.tensor_copy(into[:, :share], rows[:, :share])
+            nc.scalar.activation(into[:, share:], rows[:, share:], COPY)
             return grouped
 
         def quantize_x(s, grouped):
@@ -184,9 +186,10 @@ def tile_moe_two_glu_relu_kernel(tc, xT, w1, w3, w2, gate, offs, dst, out):
                 out_sb[:].indirect(dst_sb[:, idx]), y_sb[:], gate_sb[:, e * C : (e + 1) * C], MULT
             )
 
-        raws = load_passes(xT, 0, 2)
+        raws = load_passes(xT, 0, 1)
         nc.sync.dma_start(offs_sb[:], offs)
-        raws += load_passes(xT, 2, 2)
+        for s in range(1, PASSES):
+            raws += load_passes(xT, s, 1)
         nc.sync.dma_start(dst_sb[:], dst)
         nc.sync.dma_start(gate_row[:], gate[0:1, :].rearrange("o (n m) -> (o n) m", m=PACK))
         prev = None

@@ -48,7 +48,7 @@ def tile_moe_two_glu_relu_kernel(tc, xT, w1, w3, w2, gate, offs, dst, out):
 
         ident = keep.tile([P, P], F32, name="ident")
         make_identity(nc, ident[:])
-        out_sb = keep.tile([P, T], F32, name="out_sb")
+        out_sb = keep.tile([P, T], F32, name="out_sb", align_bytes=256)
         nc.gpsimd.memset(out_sb[:], 0.0)
 
         gate_row = keep.tile([P, PACK], F32, name="gate_row")
@@ -67,7 +67,7 @@ def tile_moe_two_glu_relu_kernel(tc, xT, w1, w3, w2, gate, offs, dst, out):
             size = 4 * shape[1] * shape[2]
             start = placed[-1] if placed[-1] + size <= ARENA else 0
             placed.append(start + size)
-            return ring.tile(shape, F32, name=f"raw{len(placed)}", offset=start)
+            return ring.tile(shape, F32, name=f"raw{len(placed)}", offset=start, align_bytes=256)
 
         def load_rows(matrix, s, j0, j1):
             raw = ring_tile([P, j1 - j0, matrix.shape[1]])

@@ -22,8 +22,8 @@ K_PASS = P * PACK
 PASSES = K // K_PASS
 HALF = H // 2
 
-X_VECTOR = 208
-W_VECTOR = 50
+X_VECTOR = 256
+W_VECTOR = 60
 W_VECTOR_END = 72
 END = 3
 LAST_VECTOR = 40
@@ -68,6 +68,9 @@ def tile_moe_two_glu_relu_kernel(tc, xT, w1, w3, w2, gate, offs, dst, out):
             start = placed[-1] if placed[-1] + size <= ARENA else 0
             placed.append(start + size)
             return ring.tile(shape, F32, name=f"raw{len(placed)}", offset=start, align_bytes=256)
+
+        def over(raw_start, shape, dtype, name):
+            return ring.tile(shape, dtype, name=name, offset=raw_start, align_bytes=256)
 
         def load_rows(matrix, s, j0, j1):
             raw = ring_tile([P, j1 - j0, matrix.shape[1]])
@@ -153,19 +156,20 @@ def tile_moe_two_glu_relu_kernel(tc, xT, w1, w3, w2, gate, offs, dst, out):
             )
             w2_codes[e] = quantize(grouped[:].rearrange("p n j -> p (n j)"), "w2", hid, E)
 
-        def hidden(a_sb, b_acc):
-            h = hid.tile([P, H], BF16, name="h", align_bytes=64, bufs=1)
+        def hidden(h, a_sb, b_acc):
             words = h[:].bitcast(F32)
             turned = psum.tile([P, 2, P], F32, name="turned", bufs=1)
             for u in range(2):
                 cols = slice(u * HALF, (u + 1) * HALF)
                 nc.vector.tensor_tensor(h[:, cols], b_acc[u][:], a_sb[:, cols], MULT)
                 nc.tensor.transpose(turned[:, u, :], words[:, u * P : (u + 1) * P], ident[:])
-            grouped = hid.tile([P, C, PACK], BF16, name="h_grouped", align_bytes=64)
+            return turned
+
+        def regroup(grouped, turned):
             nc.scalar.copy(grouped[:].bitcast(F32), turned[:].rearrange("p u r -> p r u"))
             return grouped
 
-        def project(e, h_codes):
+        def project(e, h_codes, y_sb):
             y = psum.tile([N, C], F32, name="y")
             nc.tensor.matmul_mx(
                 out=y[:],
@@ -176,7 +180,6 @@ def tile_moe_two_glu_relu_kernel(tc, xT, w1, w3, w2, gate, offs, dst, out):
                 start=True,
                 stop=True,
             )
-            y_sb = hid.tile([N, C], F32, name="y_sb")
             nc.scalar.copy(y_sb[:], y[:])
             return y_sb
 
@@ -213,6 +216,8 @@ def tile_moe_two_glu_relu_kernel(tc, xT, w1, w3, w2, gate, offs, dst, out):
         h_codes = {}
         w2_raw = {}
         w_grouped = {}
+        turned = {}
+        raw_start = {}
 
         def finish_chunk(c):
             m, e, s = chunks[c]
@@ -222,9 +227,6 @@ def tile_moe_two_glu_relu_kernel(tc, xT, w1, w3, w2, gate, offs, dst, out):
                 if s == 0:
                     acc_a[e] = psum.tile([C, H], F32, name="acc_a")
                 multiply_w(acc_a[e][:], e, s, codes[:], scales[:])
-                if s == PASSES - 1:
-                    relu_a[e] = hid.tile([C, H], F32, name="relu_a")
-                    nc.scalar.activation(relu_a[e][:], acc_a[e][:], RELU)
             else:
                 if s == 0:
                     acc_b[e] = [psum.tile([C, HALF], F32, name="acc_b") for u in range(2)]
@@ -233,21 +235,33 @@ def tile_moe_two_glu_relu_kernel(tc, xT, w1, w3, w2, gate, offs, dst, out):
                         codes, scales = quantize(flat[:, u * HALF * PACK : (u + 1) * HALF * PACK], "w", wq, 8)
                         multiply_w(acc_b[e][u][:], e, s, codes[:], scales[:])
                     quantize_w2(2, w2_raw[2])
-                    y_late.append(project(2, h_codes[2]))
+                    y_late.append(project(2, h_codes[2], hid.tile([N, C], F32, name="y_sb")))
                 else:
                     codes, scales = quantize(flat, "w", wq, 8)
                     for u in range(2):
                         cols = slice(u * HALF, (u + 1) * HALF)
                         multiply_w(acc_b[e][u][:], e, s, codes[:, cols], scales[:, cols])
-                if s == PASSES - 1:
-                    h_grouped[e] = hidden(relu_a[e], acc_b[e])
+                if c == last:
+                    h = hid.tile([P, H], BF16, name="h", align_bytes=64, bufs=1)
+                    grouped = hid.tile([P, C, PACK], BF16, name="h_grouped", align_bytes=64, bufs=1)
+                    h_grouped[e] = regroup(grouped, hidden(h, relu_a[e], acc_b[e]))
             if e == 0 and m == 1:
                 gather_x(s, 1)
+            if m == 1 and s == 1:
+                relu_a[e] = over(raw_start[c - 1], [C, H], F32, f"relu_a{e}")
+                nc.scalar.activation(relu_a[e][:], acc_a[e][:], RELU)
             if m == 0 and s == 1 and e > 0:
+                h = over(raw_start[c - 1], [P, H], BF16, f"h{e}")
+                turned[e - 1] = hidden(h, relu_a[e - 1], acc_b[e - 1])
+            if m == 0 and s == 3 and e > 0:
+                grouped = over(raw_start[c - 1], [P, C, PACK], BF16, f"h_grouped{e}")
+                h_grouped[e - 1] = regroup(grouped, turned[e - 1])
                 h_codes[e - 1] = quantize(h_grouped[e - 1][:].rearrange("p c j -> p (c j)"), "h", hid, E)
                 if e - 1 < 2:
                     quantize_w2(e - 1, w2_raw[e - 1])
-                    place(e - 1, project(e - 1, h_codes[e - 1]))
+            if m == 1 and s == 1 and e in (1, 2):
+                y_sb = over(raw_start[c - 1] + 4 * H, [N, C], F32, f"y_sb{e}")
+                place(e - 1, project(e - 1, h_codes[e - 1], y_sb))
 
         for c in range(len(chunks)):
             m, e, s = chunks[c]
@@ -259,7 +273,9 @@ def tile_moe_two_glu_relu_kernel(tc, xT, w1, w3, w2, gate, offs, dst, out):
             else:
                 if s % count == 0:
                     loaded = load_passes(w[e], s, count)
+                    loaded_start = placed[-1] - 4 * count * PACK * H
                 raw_parts = [loaded[s % count]]
+                raw_start[c] = loaded_start
             if m == 1 and s == PASSES - 1 and e == 0:
                 w2_raw[0], w2_raw[1] = load_passes(w2[0:2].rearrange("e i n -> (e i) n"), 0, 2)
             if c == last:
@@ -277,6 +293,6 @@ def tile_moe_two_glu_relu_kernel(tc, xT, w1, w3, w2, gate, offs, dst, out):
         place(2, y_late[0])
         quantize_w2(3, w2_raw[3])
         h_codes[3] = quantize(h_grouped[3][:].rearrange("p c j -> p (c j)"), "h", hid, E)
-        place(3, project(3, h_codes[3]))
+        place(3, project(3, h_codes[3], hid.tile([N, C], F32, name="y_sb")))
 
         nc.sync.dma_start(out, out_sb[:])

@@ -22,11 +22,11 @@ K_PASS = P * PACK
 PASSES = K // K_PASS
 HALF = H // 2
 
-X_VECTOR = 256
-W_VECTOR = 60
-W_VECTOR_END = 72
+X_VECTOR = 208
+W_VECTOR = 46
+W_VECTOR_END = 58
 END = 3
-LAST_VECTOR = 40
+LAST_VECTOR = 24
 GATHER = 256
 ARENA = 144 * 1024
 PASSES_A_LOAD = (2, 2, 2, 1)

@@ -122,6 +122,12 @@ def tile_moe_two_glu_relu_kernel(tc, xT, w1, w3, w2, gate, offs, dst, out):
             nc.scalar.copy(into[:, share:], rows[:, share:])
             nc.vector.tensor_copy(into[:, :share], rows[:, :share])
 
+        def interleave_plain(grouped, raw, share):
+            rows = raw.rearrange("p j (q i) -> p q j i", i=PACK)
+            into = grouped[:].rearrange("p u q e j -> p (u q e) j").rearrange("p (q i) j -> p q j i", i=PACK)
+            nc.scalar.copy(into[:, share:], rows[:, share:])
+            nc.vector.tensor_copy(into[:, :share], rows[:, :share])
+
         def interleave_last(grouped, raw, j0, j1):
             rows = raw.rearrange("p j (q u e) -> p u q j e", u=2, e=2)
             into = grouped[:].rearrange("p u q e j -> p u q j e")[:, :, :, j0:j1]
@@ -162,6 +168,19 @@ def tile_moe_two_glu_relu_kernel(tc, xT, w1, w3, w2, gate, offs, dst, out):
             for u in range(2):
                 cols = slice(u * HALF, (u + 1) * HALF)
                 nc.vector.tensor_tensor(h[:, cols], b_acc[u][:], a_sb[:, cols], MULT)
+                nc.tensor.transpose(turned[:, u, :], words[:, u * P : (u + 1) * P], ident[:])
+            return turned
+
+        def hidden_plain(h, a_sb, b_acc):
+            words = h[:].bitcast(F32)
+            turned = psum.tile([P, 2, P], F32, name="turned", bufs=1)
+            nc.vector.tensor_tensor(
+                h[:].rearrange("p (u q r) -> p q u r", u=2, r=2),
+                b_acc[:].rearrange("p (q u r) -> p q u r", u=2, r=2),
+                a_sb[:].rearrange("p (q u r) -> p q u r", u=2, r=2),
+                MULT,
+            )
+            for u in range(2):
                 nc.tensor.transpose(turned[:, u, :], words[:, u * P : (u + 1) * P], ident[:])
             return turned
 
@@ -227,6 +246,11 @@ def tile_moe_two_glu_relu_kernel(tc, xT, w1, w3, w2, gate, offs, dst, out):
                 if s == 0:
                     acc_a[e] = psum.tile([C, H], F32, name="acc_a")
                 multiply_w(acc_a[e][:], e, s, codes[:], scales[:])
+            elif e < E - 1:
+                codes, scales = quantize(flat, "w", wq, 8)
+                if s == 0:
+                    acc_b[e] = psum.tile([C, H], F32, name="acc_b")
+                multiply_w(acc_b[e][:], e, s, codes[:], scales[:])
             else:
                 if s == 0:
                     acc_b[e] = [psum.tile([C, HALF], F32, name="acc_b") for u in range(2)]
@@ -249,10 +273,17 @@ def tile_moe_two_glu_relu_kernel(tc, xT, w1, w3, w2, gate, offs, dst, out):
                 gather_x(s, 1)
             if m == 1 and s == 1:
                 relu_a[e] = over(raw_start[c - 1], [C, H], F32, f"relu_a{e}")
-                nc.scalar.activation(relu_a[e][:], acc_a[e][:], RELU)
+                if e < E - 1:
+                    nc.scalar.activation(relu_a[e][:], acc_a[e][:], RELU)
+                else:
+                    nc.scalar.activation(
+                        relu_a[e][:].rearrange("p (u q r) -> p q u r", u=2, r=2),
+                        acc_a[e][:].rearrange("p (q u r) -> p q u r", u=2, r=2),
+                        RELU,
+                    )
             if m == 0 and s == 1 and e > 0:
                 h = over(raw_start[c - 1], [P, H], BF16, f"h{e}")
-                turned[e - 1] = hidden(h, relu_a[e - 1], acc_b[e - 1])
+                turned[e - 1] = hidden_plain(h, relu_a[e - 1], acc_b[e - 1])
             if m == 0 and s == 3 and e > 0:
                 grouped = over(raw_start[c - 1], [P, C, PACK], BF16, f"h_grouped{e}")
                 h_grouped[e - 1] = regroup(grouped, turned[e - 1])
@@ -285,7 +316,9 @@ def tile_moe_two_glu_relu_kernel(tc, xT, w1, w3, w2, gate, offs, dst, out):
                 finish_chunk(c - 1)
             w_grouped[c] = wbf.tile([P, 2, P, 2, PACK], BF16, name="w_grouped", align_bytes=64)
             for raw, (j0, j1) in zip(raw_parts, parts):
-                if j0 > 0:
+                if c <= last - PASSES:
+                    interleave_plain(w_grouped[c], raw, W_VECTOR)
+                elif j0 > 0:
                     interleave_last(w_grouped[c], raw, j0, j1)
                 else:
                     interleave_w(w_grouped[c], raw, j0, j1, W_VECTOR_END if c > last - END else W_VECTOR)

@@ -12,7 +12,6 @@ U32 = mybir.dt.uint32
 U16 = mybir.dt.uint16
 U8 = mybir.dt.uint8
 FP8X4 = mybir.dt.float8_e4m3fn_x4
-COPY = mybir.ActivationFunctionType.Copy
 RELU = mybir.ActivationFunctionType.Relu
 MULT = mybir.AluOpType.mult
 
@@ -20,16 +19,14 @@ P = 128
 PACK = 4
 K_PASS = P * PACK
 PASSES = K // K_PASS
-HALF = H // 2
 
 X_VECTOR = 208
 W_VECTOR = 46
-W_VECTOR_END = 58
-END = 3
-LAST_VECTOR = 24
+W_VECTOR_END = 60
+HALF_VECTOR = 34
+QUARTER_VECTOR = 14
 GATHER = 256
-ARENA = 144 * 1024
-PASSES_A_LOAD = (2, 2, 2, 1)
+RING = 144 * 1024
 
 
 def tile_moe_two_glu_relu_kernel(tc, xT, w1, w3, w2, gate, offs, dst, out):
@@ -40,65 +37,126 @@ def tile_moe_two_glu_relu_kernel(tc, xT, w1, w3, w2, gate, offs, dst, out):
         xbf = ctx.enter_context(tc.tile_pool(name="xbf", bufs=2))
         wbf = ctx.enter_context(tc.tile_pool(name="wbf", bufs=4))
         wq = ctx.enter_context(tc.tile_pool(name="wq", bufs=8))
-        hid = ctx.enter_context(tc.tile_pool(name="hid", bufs=2))
+        hid = ctx.enter_context(tc.tile_pool(name="hid", bufs=E))
         psum = ctx.enter_context(tc.psum_pool(name="psum", bufs=2))
 
         offs_sb = keep.tile([P, E * C // 16], U16, name="offs_sb")
         dst_sb = keep.tile([P, E * C // 16], U16, name="dst_sb")
-
         ident = keep.tile([P, P], F32, name="ident")
         make_identity(nc, ident[:])
         out_sb = keep.tile([P, T], F32, name="out_sb", align_bytes=256)
         nc.gpsimd.memset(out_sb[:], 0.0)
-
         gate_row = keep.tile([P, PACK], F32, name="gate_row")
         gate_sb = keep.tile([P, E * C], F32, name="gate_sb")
-        w2_codes = {}
-
         all_codes = [keep.tile([P, T], U32, name=f"all_codes{s}", align_bytes=64) for s in range(PASSES)]
         all_scales = keep.tile([P, T], U8, name="all_scales", align_bytes=64)
         slot_codes = [keep.tile([P, E * C], U32, name=f"slot_codes{s}", align_bytes=64) for s in range(PASSES)]
         slot_scales = keep.tile([P, E * C], U8, name="slot_scales", align_bytes=64)
         nc.gpsimd.memset(all_scales[:], 0)
 
-        placed = [0]
+        ends = [0]
 
-        def ring_tile(shape):
-            size = 4 * shape[1] * shape[2]
-            start = placed[-1] if placed[-1] + size <= ARENA else 0
-            placed.append(start + size)
-            return ring.tile(shape, F32, name=f"raw{len(placed)}", offset=start, align_bytes=256)
-
-        def over(raw_start, shape, dtype, name):
-            return ring.tile(shape, dtype, name=name, offset=raw_start, align_bytes=256)
-
-        def load_rows(matrix, s, j0, j1):
-            raw = ring_tile([P, j1 - j0, matrix.shape[1]])
-            rows = matrix[s * K_PASS : (s + 1) * K_PASS, :].rearrange("(p j) i -> p j i", j=PACK)
-            nc.sync.dma_start(raw[:], rows[:, j0:j1, :])
-            return raw[:]
+        def load(rows):
+            size = 4 * rows.shape[1] * rows.shape[2]
+            start = ends[-1] if ends[-1] + size <= RING else 0
+            ends.append(start + size)
+            raw = ring.tile(list(rows.shape), F32, name=f"raw{len(ends)}", offset=start, align_bytes=256)
+            nc.sync.dma_start(raw[:], rows)
+            return raw, start
 
         def load_passes(matrix, s0, count):
-            width = matrix.shape[1]
-            raw = ring_tile([P, count, PACK * width])
             rows = matrix[s0 * K_PASS : (s0 + count) * K_PASS, :]
-            nc.sync.dma_start(raw[:], rows.rearrange("(s p j) i -> p s (j i)", p=P, j=PACK))
-            return [raw[:, s, :].rearrange("p (j i) -> p j i", j=PACK) for s in range(count)]
+            raw, start = load(rows.rearrange("(s p j) i -> p s (j i)", p=P, j=PACK))
+            return [raw[:, s, :].rearrange("p (j i) -> p j i", j=PACK) for s in range(count)], start
 
-        def spread_gate():
-            bank = psum.tile([P, PACK, P], F32, name="turned", bufs=1)
-            for m in range(PACK):
-                nc.tensor.transpose(bank[:, m, :], gate_row[:, m : m + 1].to_broadcast([P, P]), ident[:])
-            nc.scalar.copy(gate_sb[:].rearrange("p (n m) -> p n m", m=PACK), bank[:].rearrange("p m n -> p n m"))
+        def load_columns(matrix, s, q0, q1):
+            rows = matrix[s * K_PASS : (s + 1) * K_PASS, :].rearrange("(p j) i -> p j i", j=PACK)
+            return load(rows[:, :, q0 * PACK : q1 * PACK])[0][:]
 
-        def interleave_x(raw):
-            grouped = xbf.tile([P, T, PACK], BF16, name="x_grouped", align_bytes=64)
-            rows = raw.rearrange("p j (q i) -> p q j i", i=PACK)
-            into = grouped[:].rearrange("p (q i) j -> p q j i", i=PACK)
-            share = X_VECTOR // PACK
+        def behind(start, shape, dtype, name):
+            return ring.tile(shape, dtype, name=name, offset=start, align_bytes=256)
+
+        def interleave(grouped, raw, share):
+            rows = raw.rearrange("p j (g i) -> p g j i", i=PACK)
+            into = grouped[:].rearrange("p (g i) j -> p g j i", i=PACK)
+            nc.scalar.copy(into[:, share:], rows[:, share:])
+            if share:
+                nc.vector.tensor_copy(into[:, :share], rows[:, :share])
+
+        def interleave_w(grouped, raw, share):
+            rows = raw.rearrange("p j (q t) -> p q j t", t=PACK)
+            into = grouped.rearrange("p t q j -> p q j t")
+            nc.scalar.copy(into[:, share:], rows[:, share:])
             nc.vector.tensor_copy(into[:, :share], rows[:, :share])
-            nc.scalar.activation(into[:, share:], rows[:, share:], COPY)
-            return grouped
+
+        def quantize(values, name, pool):
+            width = values.shape[1] // PACK
+            codes = pool.tile([P, width], U32, name=name + "_codes", align_bytes=64)
+            scales = pool.tile([P, width], U8, name=name + "_scales", align_bytes=64)
+            nc.vector.quantize_mx(out=codes[:].bitcast(FP8X4), scales=scales[:], in_=values)
+            return codes, scales
+
+        def multiply(acc, e, s, t, codes, scales):
+            slots = slice(e * C, (e + 1) * C)
+            nc.tensor.matmul_mx(
+                out=acc[:, t, :],
+                lhsT=codes.bitcast(FP8X4),
+                lhsT_scale=scales,
+                rhs=slot_codes[s][:, slots].bitcast(FP8X4),
+                rhs_scale=slot_scales[4 * s :, slots],
+                start=s == 0 and t == 0,
+                stop=s == PASSES - 1 and t == PACK - 1,
+            )
+
+        def first_layer(acc, e, s, grouped):
+            codes, scales = quantize(grouped[:].rearrange("p t q j -> p (t q j)"), "w", wq)
+            for t in range(PACK):
+                cols = slice(t * P, (t + 1) * P)
+                multiply(acc, e, s, t, codes[:, cols], scales[:, cols])
+
+        def quantize_half(codes, scales, half, grouped, t):
+            cols = slice(t * P + half * P // 2, t * P + (half + 1) * P // 2)
+            values = grouped[:, t].rearrange("p q j -> p (q j)")
+            nc.vector.quantize_mx(out=codes[:, cols].bitcast(FP8X4), scales=scales[:, cols], in_=values)
+
+        def rectify(into, acc):
+            nc.scalar.activation(into[:], acc[:].rearrange("p t c -> p c t"), RELU)
+            return into
+
+        def hidden(h, a_sb, acc):
+            nc.vector.tensor_tensor(h[:], acc[:].rearrange("p t c -> p c t"), a_sb[:], MULT)
+            return h[:].rearrange("p c t -> p (c t)")
+
+        def quantize_w2(raw, name="w2_grouped"):
+            grouped = hid.tile([P, N, PACK], BF16, name=name, align_bytes=64, bufs=1)
+            interleave(grouped, raw, 0)
+            return quantize(grouped[:].rearrange("p n j -> p (n j)"), "w2", hid)
+
+        def second_layer(w2_q, h_q):
+            y = psum.tile([N, C], F32, name="y")
+            nc.tensor.matmul_mx(
+                out=y[:],
+                lhsT=w2_q[0][:].bitcast(FP8X4),
+                lhsT_scale=w2_q[1][:],
+                rhs=h_q[0][:].bitcast(FP8X4),
+                rhs_scale=h_q[1][:],
+                start=True,
+                stop=True,
+            )
+            return y
+
+        def place(e, y_sb):
+            idx = slice(e * C // 16, (e + 1) * C // 16)
+            nc.vector.tensor_tensor(
+                out_sb[:].indirect(dst_sb[:, idx]), y_sb[:], gate_sb[:, e * C : (e + 1) * C], MULT
+            )
+
+        def gather(s, g):
+            cols = slice(g * GATHER, (g + 1) * GATHER)
+            idx = slice(g * GATHER // 16, (g + 1) * GATHER // 16)
+            nc.vector.tensor_copy(slot_codes[s][:, cols], all_codes[s][:].indirect(offs_sb[:, idx]))
+            if s == PASSES - 1:
+                nc.vector.tensor_copy(slot_scales[:, cols], all_scales[:].indirect(offs_sb[:, idx]))
 
         def quantize_x(s, grouped):
             flat = grouped[:].rearrange("p t j -> p (t j)")
@@ -109,223 +167,94 @@ def tile_moe_two_glu_relu_kernel(tc, xT, w1, w3, w2, gate, offs, dst, out):
                     in_=flat[:, a * PACK : b * PACK],
                 )
 
-        def gather_x(s, g):
-            cols = slice(g * GATHER, (g + 1) * GATHER)
-            idx = slice(g * GATHER // 16, (g + 1) * GATHER // 16)
-            nc.vector.tensor_copy(slot_codes[s][:, cols], all_codes[s][:].indirect(offs_sb[:, idx]))
-            if s == PASSES - 1:
-                nc.vector.tensor_copy(slot_scales[:, cols], all_scales[:].indirect(offs_sb[:, idx]))
-
-        def interleave_w(grouped, raw, j0, j1, share):
-            rows = raw.rearrange("p j (q u e) -> p q j u e", u=2, e=2)
-            into = grouped[:].rearrange("p u q e j -> p q j u e")[:, :, j0:j1]
-            nc.scalar.copy(into[:, share:], rows[:, share:])
-            nc.vector.tensor_copy(into[:, :share], rows[:, :share])
-
-        def interleave_plain(grouped, raw, share):
-            rows = raw.rearrange("p j (q i) -> p q j i", i=PACK)
-            into = grouped[:].rearrange("p u q e j -> p (u q e) j").rearrange("p (q i) j -> p q j i", i=PACK)
-            nc.scalar.copy(into[:, share:], rows[:, share:])
-            nc.vector.tensor_copy(into[:, :share], rows[:, :share])
-
-        def interleave_last(grouped, raw, j0, j1):
-            rows = raw.rearrange("p j (q u e) -> p u q j e", u=2, e=2)
-            into = grouped[:].rearrange("p u q e j -> p u q j e")[:, :, :, j0:j1]
-            nc.scalar.copy(into[:, 1, LAST_VECTOR:], rows[:, 1, LAST_VECTOR:])
-            nc.vector.tensor_copy(into[:, 0], rows[:, 0])
-            nc.vector.tensor_copy(into[:, 1, :LAST_VECTOR], rows[:, 1, :LAST_VECTOR])
-
-        def quantize(values, name, pool, bufs):
-            width = values.shape[1] // PACK
-            codes = pool.tile([P, width], U32, name=name + "_codes", align_bytes=64, bufs=bufs)
-            scales = pool.tile([P, width], U8, name=name + "_scales", align_bytes=64, bufs=bufs)
-            nc.vector.quantize_mx(out=codes[:].bitcast(FP8X4), scales=scales[:], in_=values)
-            return codes, scales
-
-        def multiply_w(acc, e, s, codes, scales):
-            slots = slice(e * C, (e + 1) * C)
-            nc.tensor.matmul_mx(
-                out=acc,
-                lhsT=slot_codes[s][:, slots].bitcast(FP8X4),
-                lhsT_scale=slot_scales[4 * s :, slots],
-                rhs=codes.bitcast(FP8X4),
-                rhs_scale=scales,
-                start=s == 0,
-                stop=s == PASSES - 1,
-            )
-
-        def quantize_w2(e, raw):
-            tag = "h" if e == E - 2 else "w2_grouped"
-            grouped = hid.tile([P, N, PACK], BF16, name=tag, align_bytes=64, bufs=1)
-            nc.scalar.copy(
-                grouped[:].rearrange("p (q i) j -> p q j i", i=PACK), raw.rearrange("p j (q i) -> p q j i", i=PACK)
-            )
-            w2_codes[e] = quantize(grouped[:].rearrange("p n j -> p (n j)"), "w2", hid, E)
-
-        def hidden(h, a_sb, b_acc):
-            words = h[:].bitcast(F32)
-            turned = psum.tile([P, 2, P], F32, name="turned", bufs=1)
-            for u in range(2):
-                cols = slice(u * HALF, (u + 1) * HALF)
-                nc.vector.tensor_tensor(h[:, cols], b_acc[u][:], a_sb[:, cols], MULT)
-                nc.tensor.transpose(turned[:, u, :], words[:, u * P : (u + 1) * P], ident[:])
-            return turned
-
-        def hidden_plain(h, a_sb, b_acc):
-            words = h[:].bitcast(F32)
-            turned = psum.tile([P, 2, P], F32, name="turned", bufs=1)
-            nc.vector.tensor_tensor(
-                h[:].rearrange("p (u q r) -> p q u r", u=2, r=2),
-                b_acc[:].rearrange("p (q u r) -> p q u r", u=2, r=2),
-                a_sb[:].rearrange("p (q u r) -> p q u r", u=2, r=2),
-                MULT,
-            )
-            for u in range(2):
-                nc.tensor.transpose(turned[:, u, :], words[:, u * P : (u + 1) * P], ident[:])
-            return turned
-
-        def regroup(grouped, turned):
-            nc.scalar.copy(grouped[:].bitcast(F32), turned[:].rearrange("p u r -> p r u"))
-            return grouped
-
-        def project(e, h_codes, y_sb):
-            y = psum.tile([N, C], F32, name="y")
-            nc.tensor.matmul_mx(
-                out=y[:],
-                lhsT=w2_codes[e][0][:].bitcast(FP8X4),
-                lhsT_scale=w2_codes[e][1][:],
-                rhs=h_codes[0][:].bitcast(FP8X4),
-                rhs_scale=h_codes[1][:],
-                start=True,
-                stop=True,
-            )
-            nc.scalar.copy(y_sb[:], y[:])
-            return y_sb
-
-        def place(e, y_sb):
-            idx = slice(e * C // 16, (e + 1) * C // 16)
-            nc.vector.tensor_tensor(
-                out_sb[:].indirect(dst_sb[:, idx]), y_sb[:], gate_sb[:, e * C : (e + 1) * C], MULT
-            )
-
-        raws = load_passes(xT, 0, 1)
+        x_raw = load_passes(xT, 0, 1)[0]
         nc.sync.dma_start(offs_sb[:], offs)
         for s in range(1, PASSES):
-            raws += load_passes(xT, s, 1)
+            x_raw += load_passes(xT, s, 1)[0]
         nc.sync.dma_start(dst_sb[:], dst)
         nc.sync.dma_start(gate_row[:], gate[0:1, :].rearrange("o (n m) -> (o n) m", m=PACK))
-        prev = None
-        for s in range(PASSES):
-            if prev is not None:
-                quantize_x(s - 1, prev)
-            prev = interleave_x(raws[s])
+        x_grouped = []
+        for s in range(PASSES + 1):
             if s > 0:
-                gather_x(s - 1, 0)
-        quantize_x(PASSES - 1, prev)
-        gather_x(PASSES - 1, 0)
-        spread_gate()
+                quantize_x(s - 1, x_grouped[s - 1])
+            if s < PASSES:
+                x_grouped.append(xbf.tile([P, T, PACK], BF16, name="x_grouped", align_bytes=64))
+                interleave(x_grouped[s], x_raw[s], X_VECTOR // PACK)
+            if s > 0:
+                gather(s - 1, 0)
 
-        chunks = [(m, e, s) for e in range(E) for m in range(2) for s in range(PASSES)]
-        last = len(chunks) - 1
-        acc_a = {}
-        y_late = []
-        acc_b = {}
-        relu_a = {}
-        h_grouped = {}
-        h_codes = {}
-        w2_raw = {}
-        w_grouped = {}
-        turned = {}
-        raw_start = {}
+        bank = psum.tile([P, PACK, P], F32, name="gate_bank", bufs=1)
+        for m in range(PACK):
+            nc.tensor.transpose(bank[:, m, :], gate_row[:, m : m + 1].to_broadcast([P, P]), ident[:])
+        nc.scalar.copy(gate_sb[:].rearrange("p (n m) -> p n m", m=PACK), bank[:].rearrange("p m n -> p n m"))
 
-        def finish_chunk(c):
-            m, e, s = chunks[c]
-            flat = w_grouped.pop(c)[:].rearrange("p u q e j -> p (u q e j)")
-            if m == 0:
-                codes, scales = quantize(flat, "w", wq, 8)
-                if s == 0:
-                    acc_a[e] = psum.tile([C, H], F32, name="acc_a")
-                multiply_w(acc_a[e][:], e, s, codes[:], scales[:])
-            elif e < E - 1:
-                codes, scales = quantize(flat, "w", wq, 8)
-                if s == 0:
-                    acc_b[e] = psum.tile([C, H], F32, name="acc_b")
-                multiply_w(acc_b[e][:], e, s, codes[:], scales[:])
-            else:
-                if s == 0:
-                    acc_b[e] = [psum.tile([C, HALF], F32, name="acc_b") for u in range(2)]
-                if c == last:
-                    for u in range(2):
-                        codes, scales = quantize(flat[:, u * HALF * PACK : (u + 1) * HALF * PACK], "w", wq, 8)
-                        multiply_w(acc_b[e][u][:], e, s, codes[:], scales[:])
-                    quantize_w2(2, w2_raw[2])
-                    y_late.append(project(2, h_codes[2], hid.tile([N, C], F32, name="y_sb")))
-                else:
-                    codes, scales = quantize(flat, "w", wq, 8)
-                    for u in range(2):
-                        cols = slice(u * HALF, (u + 1) * HALF)
-                        multiply_w(acc_b[e][u][:], e, s, codes[:, cols], scales[:, cols])
-                if c == last:
-                    h = hid.tile([P, H], BF16, name="h", align_bytes=64, bufs=1)
-                    grouped = hid.tile([P, C, PACK], BF16, name="h_grouped", align_bytes=64, bufs=1)
-                    h_grouped[e] = regroup(grouped, hidden(h, relu_a[e], acc_b[e]))
+        steps = [(e, m, s) for e in range(E) for m in range(2) for s in range(PASSES)]
+        last = len(steps) - 1
+        acc, relu_a, h_q, w2_raw, w2_q, grouped, start = {}, {}, {}, {}, {}, {}, {}
+
+        def finish(c):
+            e, m, s = steps[c]
+            if s == 0:
+                acc[e, m] = psum.tile([P, PACK, C], F32, name=("acc_a", "acc_b")[m])
+            first_layer(acc[e, m], e, s, grouped.pop(c))
             if e == 0 and m == 1:
-                gather_x(s, 1)
+                gather(s, 1)
             if m == 1 and s == 1:
-                relu_a[e] = over(raw_start[c - 1], [C, H], F32, f"relu_a{e}")
-                if e < E - 1:
-                    nc.scalar.activation(relu_a[e][:], acc_a[e][:], RELU)
-                else:
-                    nc.scalar.activation(
-                        relu_a[e][:].rearrange("p (u q r) -> p q u r", u=2, r=2),
-                        acc_a[e][:].rearrange("p (q u r) -> p q u r", u=2, r=2),
-                        RELU,
-                    )
-            if m == 0 and s == 1 and e > 0:
-                h = over(raw_start[c - 1], [P, H], BF16, f"h{e}")
-                turned[e - 1] = hidden_plain(h, relu_a[e - 1], acc_b[e - 1])
-            if m == 0 and s == 3 and e > 0:
-                grouped = over(raw_start[c - 1], [P, C, PACK], BF16, f"h_grouped{e}")
-                h_grouped[e - 1] = regroup(grouped, turned[e - 1])
-                h_codes[e - 1] = quantize(h_grouped[e - 1][:].rearrange("p c j -> p (c j)"), "h", hid, E)
-                if e - 1 < 2:
-                    quantize_w2(e - 1, w2_raw[e - 1])
-            if m == 1 and s == 1 and e in (1, 2):
-                y_sb = over(raw_start[c - 1] + 4 * H, [N, C], F32, f"y_sb{e}")
-                place(e - 1, project(e - 1, h_codes[e - 1], y_sb))
+                relu_a[e] = rectify(behind(start[c - 1], [P, C, PACK], F32, f"relu_a{e}"), acc[e, 0])
+            if e > 0 and m == 0 and s == 1:
+                h = behind(start[c - 1], [P, C, PACK], BF16, f"h{e - 1}")
+                h_q[e - 1] = quantize(hidden(h, relu_a[e - 1], acc[e - 1, 1]), "h", hid)
+            if e in (1, 2) and m == 0 and s == 2:
+                w2_q[e - 1] = quantize_w2(w2_raw[e - 1])
+            if e in (1, 2) and m == 0 and s == 3:
+                y_sb = behind(start[c - 1], [N, C], F32, f"y_sb{e - 1}")
+                nc.scalar.copy(y_sb[:], second_layer(w2_q[e - 1], h_q[e - 1])[:])
+                place(e - 1, y_sb)
 
-        for c in range(len(chunks)):
-            m, e, s = chunks[c]
-            w = (w1, w3)[m]
-            parts = ((0, 2), (2, PACK)) if c == last else ((0, PACK),)
-            count = PASSES_A_LOAD[e]
-            if c == last:
-                raw_parts = [load_rows(w[e], s, j0, j1) for j0, j1 in parts]
+        for c, (e, m, s) in enumerate(steps[:last]):
+            w = (w1, w3)[m][e]
+            if c == last - 1:
+                parts = [(load_columns(w, s, q, q + P // 2), q, HALF_VECTOR) for q in (0, P // 2)]
             else:
+                count = 2 if e < E - 1 else 1
                 if s % count == 0:
-                    loaded = load_passes(w[e], s, count)
-                    loaded_start = placed[-1] - 4 * count * PACK * H
-                raw_parts = [loaded[s % count]]
-                raw_start[c] = loaded_start
-            if m == 1 and s == PASSES - 1 and e == 0:
-                w2_raw[0], w2_raw[1] = load_passes(w2[0:2].rearrange("e i n -> (e i) n"), 0, 2)
-            if c == last:
-                for late in (2, 3):
-                    w2_raw[late] = load_rows(w2[late], 0, 0, PACK)
+                    loaded, loaded_start = load_passes(w, s, count)
+                start[c] = loaded_start
+                parts = [(loaded[s % count], 0, W_VECTOR_END if c == last - 2 else W_VECTOR)]
+            if c == 2 * PASSES - 1:
+                w2_raw[0], w2_raw[1] = load_passes(w2[0:2].rearrange("e i n -> (e i) n"), 0, 2)[0]
             if c > 0:
-                finish_chunk(c - 1)
-            w_grouped[c] = wbf.tile([P, 2, P, 2, PACK], BF16, name="w_grouped", align_bytes=64)
-            for raw, (j0, j1) in zip(raw_parts, parts):
-                if c <= last - PASSES:
-                    interleave_plain(w_grouped[c], raw, W_VECTOR)
-                elif j0 > 0:
-                    interleave_last(w_grouped[c], raw, j0, j1)
-                else:
-                    interleave_w(w_grouped[c], raw, j0, j1, W_VECTOR_END if c > last - END else W_VECTOR)
-        finish_chunk(last)
-        place(2, y_late[0])
-        quantize_w2(3, w2_raw[3])
-        h_codes[3] = quantize(h_grouped[3][:].rearrange("p c j -> p (c j)"), "h", hid, E)
-        place(3, project(3, h_codes[3], hid.tile([N, C], F32, name="y_sb")))
+                finish(c - 1)
+            grouped[c] = wbf.tile([P, PACK, P, PACK], BF16, name="w_grouped", align_bytes=64)
+            for raw, q, share in parts:
+                interleave_w(grouped[c][:, :, q : q + raw.shape[2] // PACK], raw, share)
+
+        pieces = [load_columns(w3[3], 3, q0, q1) for q0, q1 in ((0, 64), (64, 96), (96, 128))]
+        for late in (2, 3):
+            w2_raw[late] = load_passes(w2[late], 0, 1)[0][0]
+        halves = [hid.tile([P, PACK, P // 2, PACK], BF16, name="w_half", align_bytes=64, bufs=2) for half in range(2)]
+        codes = wq.tile([P, H], U32, name="w_codes", align_bytes=64)
+        scales = wq.tile([P, H], U8, name="w_scales", align_bytes=64)
+        finish(last - 1)
+        interleave_w(halves[0][:], pieces[0], HALF_VECTOR)
+        interleave_w(halves[1][:, :, :32], pieces[1], QUARTER_VECTOR)
+        for t in range(PACK):
+            quantize_half(codes, scales, 0, halves[0], t)
+        interleave_w(halves[1][:, :, 32:], pieces[2], QUARTER_VECTOR)
+        for t in range(PACK):
+            quantize_half(codes, scales, 1, halves[1], t)
+            cols = slice(t * P, (t + 1) * P)
+            multiply(acc[3, 1], 3, 3, t, codes[:, cols], scales[:, cols])
+
+        w2_q[2] = quantize_w2(w2_raw[2], "h")
+        y2 = second_layer(w2_q[2], h_q[2])
+        w2_q[3] = quantize_w2(w2_raw[3])
+        h = hidden(hid.tile([P, C, PACK], BF16, name="h", align_bytes=64, bufs=1), relu_a[3], acc[3, 1])
+        y_sb = [hid.tile([N, C], F32, name="y_sb", bufs=2) for late in (2, 3)]
+        nc.vector.tensor_copy(y_sb[0][:], y2[:])
+        h_q[3] = quantize(h, "h", hid)
+        place(2, y_sb[0])
+        nc.scalar.copy(y_sb[1][:], second_layer(w2_q[3], h_q[3])[:])
+        place(3, y_sb[1])
 
         nc.sync.dma_start(out, out_sb[:])

@@ -84,10 +84,10 @@ def tile_moe_two_glu_relu_kernel(tc, xT, w1, w3, w2, gate, offs, dst, out):
                 nc.vector.tensor_copy(into[:, :share], rows[:, :share])
 
         def interleave_w(grouped, raw, share):
-            rows = raw.rearrange("p j (q t) -> p q j t", t=PACK)
-            into = grouped.rearrange("p t q j -> p q j t")
-            nc.scalar.copy(into[:, share:], rows[:, share:])
-            nc.vector.tensor_copy(into[:, :share], rows[:, :share])
+            rows = raw.rearrange("p j (q u r) -> p u q j r", u=2, r=2)
+            into = grouped.rearrange("p (u r) q j -> p u q j r", u=2)
+            nc.scalar.copy(into[:, :, share:], rows[:, :, share:])
+            nc.vector.tensor_copy(into[:, :, :share], rows[:, :, :share])
 
         def quantize(values, name, pool):
             width = values.shape[1] // PACK
@@ -120,11 +120,12 @@ def tile_moe_two_glu_relu_kernel(tc, xT, w1, w3, w2, gate, offs, dst, out):
             nc.vector.quantize_mx(out=codes[:, cols].bitcast(FP8X4), scales=scales[:, cols], in_=values)
 
         def rectify(into, acc):
-            nc.scalar.activation(into[:], acc[:].rearrange("p t c -> p c t"), RELU)
+            nc.scalar.activation(into[:], acc[:].rearrange("p t (c r) -> p c t r", r=2), RELU)
             return into
 
         def hidden(h, a_sb, acc):
-            nc.vector.tensor_tensor(h[:], acc[:].rearrange("p t c -> p c t"), a_sb[:], MULT)
+            into = h[:].rearrange("p (c r) t -> p c t r", r=2)
+            nc.vector.tensor_tensor(into, acc[:].rearrange("p t (c r) -> p c t r", r=2), a_sb[:], MULT)
             return h[:].rearrange("p c t -> p (c t)")
 
         def quantize_w2(raw, name="w2_grouped"):
@@ -200,7 +201,7 @@ def tile_moe_two_glu_relu_kernel(tc, xT, w1, w3, w2, gate, offs, dst, out):
             if e == 0 and m == 1:
                 gather(s, 1)
             if m == 1 and s == 1:
-                relu_a[e] = rectify(behind(start[c - 1], [P, C, PACK], F32, f"relu_a{e}"), acc[e, 0])
+                relu_a[e] = rectify(behind(start[c - 1], [P, C // 2, PACK, 2], F32, f"relu_a{e}"), acc[e, 0])
             if e > 0 and m == 0 and s == 1:
                 h = behind(start[c - 1], [P, C, PACK], BF16, f"h{e - 1}")
                 h_q[e - 1] = quantize(hidden(h, relu_a[e - 1], acc[e - 1, 1]), "h", hid)

@@ -78,7 +78,7 @@ def tile_moe_two_glu_relu_kernel(tc, xT, w1, w3, w2, gate, offs, dst, out):
 
         def interleave(grouped, raw, share):
             rows = raw.rearrange("p j (g i) -> p g j i", i=PACK)
-            into = grouped[:].rearrange("p (g i) j -> p g j i", i=PACK)
+            into = grouped.rearrange("p (g i) j -> p g j i", i=PACK)
             nc.scalar.copy(into[:, share:], rows[:, share:])
             if share:
                 nc.vector.tensor_copy(into[:, :share], rows[:, :share])
@@ -114,6 +114,32 @@ def tile_moe_two_glu_relu_kernel(tc, xT, w1, w3, w2, gate, offs, dst, out):
                 cols = slice(t * P, (t + 1) * P)
                 multiply(acc, e, s, t, codes[:, cols], scales[:, cols])
 
+        def first_layer_early(acc, e, s, grouped):
+            codes, scales = quantize(grouped[:].rearrange("p t q j -> p (t q j)"), "w", wq)
+            slots = slice(e * C, (e + 1) * C)
+            nc.tensor.matmul_mx(
+                out=acc[:].rearrange("p t c -> p (t c)"),
+                lhsT=slot_codes[s][:, slots].bitcast(FP8X4),
+                lhsT_scale=slot_scales[4 * s :, slots],
+                rhs=codes[:].bitcast(FP8X4),
+                rhs_scale=scales[:],
+                start=s == 0,
+                stop=s == PASSES - 1,
+            )
+
+        def hidden_early(h, a_sb, acc):
+            turned = psum.tile([P, 2, P], F32, name="turned", bufs=1)
+            nc.vector.tensor_tensor(
+                h[:].rearrange("p (u q r) -> p q u r", u=2, r=2),
+                acc[:].rearrange("p t (g u r) -> p (t g) u r", u=2, r=2),
+                a_sb[:].rearrange("p (q u r) -> p q u r", u=2, r=2),
+                MULT,
+            )
+            words = h[:].bitcast(F32)
+            for u in range(2):
+                nc.tensor.transpose(turned[:, u, :], words[:, u * P : (u + 1) * P], ident[:])
+            return turned
+
         def quantize_half(codes, scales, half, grouped, t):
             cols = slice(t * P + half * P // 2, t * P + (half + 1) * P // 2)
             values = grouped[:, t].rearrange("p q j -> p (q j)")
@@ -130,7 +156,7 @@ def tile_moe_two_glu_relu_kernel(tc, xT, w1, w3, w2, gate, offs, dst, out):
 
         def quantize_w2(raw, name="w2_grouped"):
             grouped = hid.tile([P, N, PACK], BF16, name=name, align_bytes=64, bufs=1)
-            interleave(grouped, raw, 0)
+            interleave(grouped[:], raw, 0)
             return quantize(grouped[:].rearrange("p n j -> p (n j)"), "w2", hid)
 
         def second_layer(w2_q, h_q):
@@ -180,35 +206,43 @@ def tile_moe_two_glu_relu_kernel(tc, xT, w1, w3, w2, gate, offs, dst, out):
                 quantize_x(s - 1, x_grouped[s - 1])
             if s < PASSES:
                 x_grouped.append(xbf.tile([P, T, PACK], BF16, name="x_grouped", align_bytes=64))
-                interleave(x_grouped[s], x_raw[s], X_VECTOR // PACK)
+                interleave(x_grouped[s][:], x_raw[s], X_VECTOR // PACK)
             if s > 0:
                 gather(s - 1, 0)
 
-        bank = psum.tile([P, PACK, P], F32, name="gate_bank", bufs=1)
+        bank = psum.tile([P, PACK, P], F32, name="turned", bufs=1)
         for m in range(PACK):
             nc.tensor.transpose(bank[:, m, :], gate_row[:, m : m + 1].to_broadcast([P, P]), ident[:])
         nc.scalar.copy(gate_sb[:].rearrange("p (n m) -> p n m", m=PACK), bank[:].rearrange("p m n -> p n m"))
 
         steps = [(e, m, s) for e in range(E) for m in range(2) for s in range(PASSES)]
         last = len(steps) - 1
-        acc, relu_a, h_q, w2_raw, w2_q, grouped, start = {}, {}, {}, {}, {}, {}, {}
+        acc, relu_a, turned, h_q, w2_raw, w2_q, grouped, start = {}, {}, {}, {}, {}, {}, {}, {}
 
         def finish(c):
             e, m, s = steps[c]
             if s == 0:
                 acc[e, m] = psum.tile([P, PACK, C], F32, name=("acc_a", "acc_b")[m])
-            first_layer(acc[e, m], e, s, grouped.pop(c))
+            (first_layer if e == E - 1 else first_layer_early)(acc[e, m], e, s, grouped.pop(c))
             if e == 0 and m == 1:
                 gather(s, 1)
-            if m == 1 and s == 1:
+            if e < E - 1 and m == 1 and s == 1:
+                relu_a[e] = behind(start[c - 1], [C, H], F32, f"relu_a{e}")
+                nc.scalar.activation(relu_a[e][:], acc[e, 0][:].rearrange("p t c -> p (t c)"), RELU)
+            if e == E - 1 and m == 1 and s == 1:
                 relu_a[e] = rectify(behind(start[c - 1], [P, C // 2, PACK, 2], F32, f"relu_a{e}"), acc[e, 0])
             if e > 0 and m == 0 and s == 1:
-                h = behind(start[c - 1], [P, C, PACK], BF16, f"h{e - 1}")
-                h_q[e - 1] = quantize(hidden(h, relu_a[e - 1], acc[e - 1, 1]), "h", hid)
-            if e in (1, 2) and m == 0 and s == 2:
-                w2_q[e - 1] = quantize_w2(w2_raw[e - 1])
+                h = behind(start[c - 1], [C, H], BF16, f"h{e - 1}")
+                turned[e - 1] = hidden_early(h, relu_a[e - 1], acc[e - 1, 1])
+            if e > 0 and m == 0 and s == 3:
+                regrouped = behind(start[c - 1], [P, C * PACK], BF16, f"h_grouped{e - 1}")
+                words = regrouped[:].bitcast(F32).rearrange("p (c u) -> p c u", u=2)
+                nc.scalar.copy(words, turned[e - 1][:].rearrange("p u c -> p c u"))
+                h_q[e - 1] = quantize(regrouped[:], "h", hid)
             if e in (1, 2) and m == 0 and s == 3:
-                y_sb = behind(start[c - 1], [N, C], F32, f"y_sb{e - 1}")
+                w2_q[e - 1] = quantize_w2(w2_raw[e - 1])
+            if e in (1, 2) and m == 1 and s == 1:
+                y_sb = behind(start[c - 1] + 4 * H, [N, C], F32, f"y_sb{e - 1}")
                 nc.scalar.copy(y_sb[:], second_layer(w2_q[e - 1], h_q[e - 1])[:])
                 place(e - 1, y_sb)
 
@@ -228,7 +262,10 @@ def tile_moe_two_glu_relu_kernel(tc, xT, w1, w3, w2, gate, offs, dst, out):
                 finish(c - 1)
             grouped[c] = wbf.tile([P, PACK, P, PACK], BF16, name="w_grouped", align_bytes=64)
             for raw, q, share in parts:
-                interleave_w(grouped[c][:, :, q : q + raw.shape[2] // PACK], raw, share)
+                if e < E - 1:
+                    interleave(grouped[c][:].rearrange("p t q j -> p (t q) j"), raw, share)
+                else:
+                    interleave_w(grouped[c][:, :, q : q + raw.shape[2] // PACK], raw, share)
 
         pieces = [load_columns(w3[3], 3, q0, q1) for q0, q1 in ((0, 64), (64, 96), (96, 128))]
         for late in (2, 3):

@@ -22,9 +22,8 @@ PASSES = K // K_PASS
 
 X_VECTOR = 208
 W_VECTOR = 46
-W_VECTOR_END = 60
-HALF_VECTOR = 34
-QUARTER_VECTOR = 14
+W_VECTOR_END = 64
+LAST_VECTOR = 32
 GATHER = 256
 RING = 144 * 1024
 
@@ -69,9 +68,9 @@ def tile_moe_two_glu_relu_kernel(tc, xT, w1, w3, w2, gate, offs, dst, out):
             raw, start = load(rows.rearrange("(s p j) i -> p s (j i)", p=P, j=PACK))
             return [raw[:, s, :].rearrange("p (j i) -> p j i", j=PACK) for s in range(count)], start
 
-        def load_columns(matrix, s, q0, q1):
+        def load_rows(matrix, s, j0, j1):
             rows = matrix[s * K_PASS : (s + 1) * K_PASS, :].rearrange("(p j) i -> p j i", j=PACK)
-            return load(rows[:, :, q0 * PACK : q1 * PACK])[0][:]
+            return load(rows[:, j0:j1, :])[0][:]
 
         def behind(start, shape, dtype, name):
             return ring.tile(shape, dtype, name=name, offset=start, align_bytes=256)
@@ -139,11 +138,6 @@ def tile_moe_two_glu_relu_kernel(tc, xT, w1, w3, w2, gate, offs, dst, out):
             for u in range(2):
                 nc.tensor.transpose(turned[:, u, :], words[:, u * P : (u + 1) * P], ident[:])
             return turned
-
-        def quantize_half(codes, scales, half, grouped, t):
-            cols = slice(t * P + half * P // 2, t * P + (half + 1) * P // 2)
-            values = grouped[:, t].rearrange("p q j -> p (q j)")
-            nc.vector.quantize_mx(out=codes[:, cols].bitcast(FP8X4), scales=scales[:, cols], in_=values)
 
         def rectify(into, acc):
             nc.scalar.activation(into[:], acc[:].rearrange("p t (c r) -> p c t r", r=2), RELU)
@@ -248,41 +242,34 @@ def tile_moe_two_glu_relu_kernel(tc, xT, w1, w3, w2, gate, offs, dst, out):
 
         for c, (e, m, s) in enumerate(steps[:last]):
             w = (w1, w3)[m][e]
-            if c == last - 1:
-                parts = [(load_columns(w, s, q, q + P // 2), q, HALF_VECTOR) for q in (0, P // 2)]
-            else:
-                count = 2 if e < E - 1 else 1
-                if s % count == 0:
-                    loaded, loaded_start = load_passes(w, s, count)
-                start[c] = loaded_start
-                parts = [(loaded[s % count], 0, W_VECTOR_END if c == last - 2 else W_VECTOR)]
+            count = 2 if e < E - 1 else 1
+            if s % count == 0:
+                loaded, loaded_start = load_passes(w, s, count)
+            start[c] = loaded_start
             if c == 2 * PASSES - 1:
                 w2_raw[0], w2_raw[1] = load_passes(w2[0:2].rearrange("e i n -> (e i) n"), 0, 2)[0]
             if c > 0:
                 finish(c - 1)
             grouped[c] = wbf.tile([P, PACK, P, PACK], BF16, name="w_grouped", align_bytes=64)
-            for raw, q, share in parts:
-                if e < E - 1:
-                    interleave(grouped[c][:].rearrange("p t q j -> p (t q) j"), raw, share)
-                else:
-                    interleave_w(grouped[c][:, :, q : q + raw.shape[2] // PACK], raw, share)
+            if e < E - 1:
+                interleave(grouped[c][:].rearrange("p t q j -> p (t q) j"), loaded[s % count], W_VECTOR)
+            else:
+                interleave_w(grouped[c][:], loaded[0], W_VECTOR_END if c >= last - 2 else W_VECTOR)
 
-        pieces = [load_columns(w3[3], 3, q0, q1) for q0, q1 in ((0, 64), (64, 96), (96, 128))]
+        pairs = [load_rows(w3[3], 3, j, j + 2) for j in (0, 2)]
         for late in (2, 3):
             w2_raw[late] = load_passes(w2[late], 0, 1)[0][0]
-        halves = [hid.tile([P, PACK, P // 2, PACK], BF16, name="w_half", align_bytes=64, bufs=2) for half in range(2)]
-        codes = wq.tile([P, H], U32, name="w_codes", align_bytes=64)
-        scales = wq.tile([P, H], U8, name="w_scales", align_bytes=64)
         finish(last - 1)
-        interleave_w(halves[0][:], pieces[0], HALF_VECTOR)
-        interleave_w(halves[1][:, :, :32], pieces[1], QUARTER_VECTOR)
+        final = wbf.tile([P, PACK, P, PACK], BF16, name="w_grouped", align_bytes=64)
+        interleave_w(final[:, :, :, 0:2], pairs[0], W_VECTOR_END)
+        rows = pairs[1].rearrange("p j (q u r) -> p u q j r", u=2, r=2)
+        into = final[:, :, :, 2:4].rearrange("p (u r) q j -> p u q j r", u=2)
+        nc.scalar.copy(into[:, 1, LAST_VECTOR:], rows[:, 1, LAST_VECTOR:])
+        nc.vector.tensor_copy(into[:, 0], rows[:, 0])
+        nc.vector.tensor_copy(into[:, 1, :LAST_VECTOR], rows[:, 1, :LAST_VECTOR])
         for t in range(PACK):
-            quantize_half(codes, scales, 0, halves[0], t)
-        interleave_w(halves[1][:, :, 32:], pieces[2], QUARTER_VECTOR)
-        for t in range(PACK):
-            quantize_half(codes, scales, 1, halves[1], t)
-            cols = slice(t * P, (t + 1) * P)
-            multiply(acc[3, 1], 3, 3, t, codes[:, cols], scales[:, cols])
+            codes, scales = quantize(final[:, t].rearrange("p q j -> p (q j)"), "w", wq)
+            multiply(acc[3, 1], 3, 3, t, codes[:], scales[:])
 
         w2_q[2] = quantize_w2(w2_raw[2], "h")
         y2 = second_layer(w2_q[2], h_q[2])

@@ -23,7 +23,7 @@ PASSES = K // K_PASS
 X_VECTOR = 208
 W_VECTOR = 46
 W_VECTOR_END = 64
-LAST_VECTOR = 32
+LAST_VECTOR = 80
 GATHER = 256
 RING = 144 * 1024
 
@@ -264,9 +264,9 @@ def tile_moe_two_glu_relu_kernel(tc, xT, w1, w3, w2, gate, offs, dst, out):
         interleave_w(final[:, :, :, 0:2], pairs[0], W_VECTOR_END)
         rows = pairs[1].rearrange("p j (q u r) -> p u q j r", u=2, r=2)
         into = final[:, :, :, 2:4].rearrange("p (u r) q j -> p u q j r", u=2)
-        nc.scalar.copy(into[:, 1, LAST_VECTOR:], rows[:, 1, LAST_VECTOR:])
-        nc.vector.tensor_copy(into[:, 0], rows[:, 0])
-        nc.vector.tensor_copy(into[:, 1, :LAST_VECTOR], rows[:, 1, :LAST_VECTOR])
+        for u in range(2):
+            nc.scalar.copy(into[:, u, LAST_VECTOR:], rows[:, u, LAST_VECTOR:])
+            nc.vector.tensor_copy(into[:, u, :LAST_VECTOR], rows[:, u, :LAST_VECTOR])
         for t in range(PACK):
             codes, scales = quantize(final[:, t].rearrange("p q j -> p (q j)"), "w", wq)
             multiply(acc[3, 1], 3, 3, t, codes[:], scales[:])

@@ -217,14 +217,20 @@ def tile_moe_two_glu_relu_kernel(tc, xT, w1, w3, w2, gate, offs, dst, out):
             e, m, s = steps[c]
             if s == 0:
                 acc[e, m] = psum.tile([P, PACK, C], F32, name=("acc_a", "acc_b")[m])
-            (first_layer if e == E - 1 else first_layer_early)(acc[e, m], e, s, grouped.pop(c))
+            (first_layer if c > last - PASSES else first_layer_early)(acc[e, m], e, s, grouped.pop(c))
             if e == 0 and m == 1:
                 gather(s, 1)
             if e < E - 1 and m == 1 and s == 1:
                 relu_a[e] = behind(start[c - 1], [C, H], F32, f"relu_a{e}")
                 nc.scalar.activation(relu_a[e][:], acc[e, 0][:].rearrange("p t c -> p (t c)"), RELU)
+            if e == E - 1 and m == 1 and s == 0:
+                a_sb = behind(start[c - 1], [C, PACK, P], F32, "a_by_sets")
+                nc.scalar.copy(a_sb[:], acc[e, 0][:].rearrange("p t (g u) -> p u (t g)", u=PACK))
+                turned[e] = psum.tile([P, PACK, C], F32, name="turned", bufs=1)
+                for t in range(PACK):
+                    nc.tensor.transpose(turned[e][:, t, :], a_sb[:, t, :], ident[:])
             if e == E - 1 and m == 1 and s == 1:
-                relu_a[e] = rectify(behind(start[c - 1], [P, C // 2, PACK, 2], F32, f"relu_a{e}"), acc[e, 0])
+                relu_a[e] = rectify(behind(start[c - 1], [P, C // 2, PACK, 2], F32, f"relu_a{e}"), turned[e])
             if e > 0 and m == 0 and s == 1:
                 h = behind(start[c - 1], [C, H], BF16, f"h{e - 1}")
                 turned[e - 1] = hidden_early(h, relu_a[e - 1], acc[e - 1, 1])
@@ -251,10 +257,10 @@ def tile_moe_two_glu_relu_kernel(tc, xT, w1, w3, w2, gate, offs, dst, out):
             if c > 0:
                 finish(c - 1)
             grouped[c] = wbf.tile([P, PACK, P, PACK], BF16, name="w_grouped", align_bytes=64)
-            if e < E - 1:
+            if c <= last - PASSES:
                 interleave(grouped[c][:].rearrange("p t q j -> p (t q) j"), loaded[s % count], W_VECTOR)
             else:
-                interleave_w(grouped[c][:], loaded[0], W_VECTOR_END if c >= last - 2 else W_VECTOR)
+                interleave_w(grouped[c][:], loaded[0], W_VECTOR_END)
 
         pairs = [load_rows(w3[3], 3, j, j + 2) for j in (0, 2)]
         for late in (2, 3):

@@ -107,11 +107,28 @@ def tile_moe_two_glu_relu_kernel(tc, xT, w1, w3, w2, gate, offs, dst, out):
                 stop=s == PASSES - 1 and t == PACK - 1,
             )
 
+        moving = {}
+
+        def warm_up(left, right):
+            unread = psum.tile([P, H], F32, name="unread", bufs=1)
+            nc.tensor.matmul_mx(
+                out=unread[:],
+                lhsT=left[0].bitcast(FP8X4),
+                lhsT_scale=left[1],
+                rhs=right[0][:].bitcast(FP8X4),
+                rhs_scale=right[1][:],
+                start=True,
+                stop=True,
+            )
+
         def first_layer(acc, e, s, grouped):
             codes, scales = quantize(grouped[:].rearrange("p t q j -> p (t q j)"), "w", wq)
             for t in range(PACK):
                 cols = slice(t * P, (t + 1) * P)
                 multiply(acc, e, s, t, codes[:, cols], scales[:, cols])
+            moving[s] = codes, scales
+            for repeat in range((0, 2, 1)[s]):
+                warm_up((slot_codes[0][:, :C], slot_scales[:, :C]), moving[s])
 
         def first_layer_early(acc, e, s, grouped):
             codes, scales = quantize(grouped[:].rearrange("p t q j -> p (t q j)"), "w", wq)
@@ -277,8 +294,10 @@ def tile_moe_two_glu_relu_kernel(tc, xT, w1, w3, w2, gate, offs, dst, out):
             codes, scales = quantize(final[:, t].rearrange("p q j -> p (q j)"), "w", wq)
             multiply(acc[3, 1], 3, 3, t, codes[:], scales[:])
 
+        warm_up((codes[:], scales[:]), moving[2])
         w2_q[2] = quantize_w2(w2_raw[2], "h")
         y2 = second_layer(w2_q[2], h_q[2])
+        warm_up((w2_q[2][0][:], w2_q[2][1][:]), moving[2])
         w2_q[3] = quantize_w2(w2_raw[3])
         h = hidden(hid.tile([P, C, PACK], BF16, name="h", align_bytes=64, bufs=1), relu_a[3], acc[3, 1])
         y_sb = [hid.tile([N, C], F32, name="y_sb", bufs=2) for late in (2, 3)]

@@ -26,6 +26,7 @@ W_VECTOR_END = 64
 LAST_VECTOR = 80
 GATHER = 256
 RING = 144 * 1024
+PAGE = 4096
 
 
 def tile_moe_two_glu_relu_kernel(tc, xT, w1, w3, w2, gate, offs, dst, out):
@@ -56,10 +57,10 @@ def tile_moe_two_glu_relu_kernel(tc, xT, w1, w3, w2, gate, offs, dst, out):
         ends = [0]
 
         def load(rows):
-            size = 4 * rows.shape[1] * rows.shape[2]
+            size = -(-4 * rows.shape[1] * rows.shape[2] // PAGE) * PAGE
             start = ends[-1] if ends[-1] + size <= RING else 0
             ends.append(start + size)
-            raw = ring.tile(list(rows.shape), F32, name=f"raw{len(ends)}", offset=start, align_bytes=256)
+            raw = ring.tile(list(rows.shape), F32, name=f"raw{len(ends)}", offset=start, align_bytes=PAGE)
             nc.sync.dma_start(raw[:], rows)
             return raw, start
 

@@ -23,7 +23,9 @@ PASSES = K // K_PASS
 X_VECTOR = 208
 W_VECTOR = 46
 W_VECTOR_END = 64
-LAST_VECTOR = 80
+BEFORE_LAST_VECTOR = 84
+FIRST_ROWS_VECTOR = 52
+LAST_VECTOR = (84, 76)
 GATHER = 256
 RING = 144 * 1024
 PAGE = 4096
@@ -108,28 +110,11 @@ def tile_moe_two_glu_relu_kernel(tc, xT, w1, w3, w2, gate, offs, dst, out):
                 stop=s == PASSES - 1 and t == PACK - 1,
             )
 
-        moving = {}
-
-        def warm_up(left, right):
-            unread = psum.tile([P, H], F32, name="unread", bufs=1)
-            nc.tensor.matmul_mx(
-                out=unread[:],
-                lhsT=left[0].bitcast(FP8X4),
-                lhsT_scale=left[1],
-                rhs=right[0][:].bitcast(FP8X4),
-                rhs_scale=right[1][:],
-                start=True,
-                stop=True,
-            )
-
         def first_layer(acc, e, s, grouped):
             codes, scales = quantize(grouped[:].rearrange("p t q j -> p (t q j)"), "w", wq)
             for t in range(PACK):
                 cols = slice(t * P, (t + 1) * P)
                 multiply(acc, e, s, t, codes[:, cols], scales[:, cols])
-            moving[s] = codes, scales
-            for repeat in range((0, 2, 1)[s]):
-                warm_up((slot_codes[0][:, :C], slot_scales[:, :C]), moving[s])
 
         def first_layer_early(acc, e, s, grouped):
             codes, scales = quantize(grouped[:].rearrange("p t q j -> p (t q j)"), "w", wq)
@@ -278,27 +263,25 @@ def tile_moe_two_glu_relu_kernel(tc, xT, w1, w3, w2, gate, offs, dst, out):
             if c <= last - PASSES:
                 interleave(grouped[c][:].rearrange("p t q j -> p (t q) j"), loaded[s % count], W_VECTOR)
             else:
-                interleave_w(grouped[c][:], loaded[0], W_VECTOR_END)
+                interleave_w(grouped[c][:], loaded[0], BEFORE_LAST_VECTOR if c == last - 1 else W_VECTOR_END)
 
         pairs = [load_rows(w3[3], 3, j, j + 2) for j in (0, 2)]
         for late in (2, 3):
             w2_raw[late] = load_passes(w2[late], 0, 1)[0][0]
         finish(last - 1)
         final = wbf.tile([P, PACK, P, PACK], BF16, name="w_grouped", align_bytes=64)
-        interleave_w(final[:, :, :, 0:2], pairs[0], W_VECTOR_END)
+        interleave_w(final[:, :, :, 0:2], pairs[0], FIRST_ROWS_VECTOR)
         rows = pairs[1].rearrange("p j (q u r) -> p u q j r", u=2, r=2)
         into = final[:, :, :, 2:4].rearrange("p (u r) q j -> p u q j r", u=2)
         for u in range(2):
-            nc.scalar.copy(into[:, u, LAST_VECTOR:], rows[:, u, LAST_VECTOR:])
-            nc.vector.tensor_copy(into[:, u, :LAST_VECTOR], rows[:, u, :LAST_VECTOR])
+            nc.scalar.copy(into[:, u, LAST_VECTOR[u] :], rows[:, u, LAST_VECTOR[u] :])
+            nc.vector.tensor_copy(into[:, u, : LAST_VECTOR[u]], rows[:, u, : LAST_VECTOR[u]])
         for t in range(PACK):
             codes, scales = quantize(final[:, t].rearrange("p q j -> p (q j)"), "w", wq)
             multiply(acc[3, 1], 3, 3, t, codes[:], scales[:])
 
-        warm_up((codes[:], scales[:]), moving[2])
         w2_q[2] = quantize_w2(w2_raw[2], "h")
         y2 = second_layer(w2_q[2], h_q[2])
-        warm_up((w2_q[2][0][:], w2_q[2][1][:]), moving[2])
         w2_q[3] = quantize_w2(w2_raw[3])
         h = hidden(hid.tile([P, C, PACK], BF16, name="h", align_bytes=64, bufs=1), relu_a[3], acc[3, 1])
         y_sb = [hid.tile([N, C], F32, name="y_sb", bufs=2) for late in (2, 3)]

@@ -142,15 +142,6 @@ def tile_moe_two_glu_relu_kernel(tc, xT, w1, w3, w2, gate, offs, dst, out):
                 nc.tensor.transpose(turned[:, u, :], words[:, u * P : (u + 1) * P], ident[:])
             return turned
 
-        def rectify(into, acc):
-            nc.scalar.activation(into[:], acc[:].rearrange("p t (c r) -> p c t r", r=2), RELU)
-            return into
-
-        def hidden(h, a_sb, acc):
-            into = h[:].rearrange("p (c r) t -> p c t r", r=2)
-            nc.vector.tensor_tensor(into, acc[:].rearrange("p t (c r) -> p c t r", r=2), a_sb[:], MULT)
-            return h[:].rearrange("p c t -> p (c t)")
-
         def quantize_w2(raw, name="w2_grouped"):
             grouped = hid.tile([P, N, PACK], BF16, name=name, align_bytes=64, bufs=1)
             interleave(grouped[:], raw, 0)
@@ -233,7 +224,11 @@ def tile_moe_two_glu_relu_kernel(tc, xT, w1, w3, w2, gate, offs, dst, out):
                 for t in range(PACK):
                     nc.tensor.transpose(turned[e][:, t, :], a_sb[:, t, :], ident[:])
             if e == E - 1 and m == 1 and s == 1:
-                relu_a[e] = rectify(behind(start[c - 1], [P, C // 2, PACK, 2], F32, f"relu_a{e}"), turned[e])
+                relu_start = [start[c - 1] + half * 2 * H for half in range(2)]
+                by_pairs = turned[e][:].rearrange("p t (c r) -> p c t r", r=2)
+                for half in range(2):
+                    relu_a[e, half] = behind(relu_start[half], [P, C // 4, PACK, 2], F32, f"relu_a{e}_{half}")
+                    nc.scalar.activation(relu_a[e, half][:], by_pairs[:, half * C // 4 : (half + 1) * C // 4], RELU)
             if e > 0 and m == 0 and s == 1:
                 h = behind(start[c - 1], [C, H], BF16, f"h{e - 1}")
                 turned[e - 1] = hidden_early(h, relu_a[e - 1], acc[e - 1, 1])
@@ -266,8 +261,9 @@ def tile_moe_two_glu_relu_kernel(tc, xT, w1, w3, w2, gate, offs, dst, out):
                 interleave_w(grouped[c][:], loaded[0], BEFORE_LAST_VECTOR if c == last - 1 else W_VECTOR_END)
 
         pairs = [load_rows(w3[3], 3, j, j + 2) for j in (0, 2)]
+        w2_start = {}
         for late in (2, 3):
-            w2_raw[late] = load_passes(w2[late], 0, 1)[0][0]
+            (w2_raw[late],), w2_start[late] = load_passes(w2[late], 0, 1)
         finish(last - 1)
         final = wbf.tile([P, PACK, P, PACK], BF16, name="w_grouped", align_bytes=64)
         interleave_w(final[:, :, :, 0:2], pairs[0], FIRST_ROWS_VECTOR)
@@ -280,13 +276,34 @@ def tile_moe_two_glu_relu_kernel(tc, xT, w1, w3, w2, gate, offs, dst, out):
             codes, scales = quantize(final[:, t].rearrange("p q j -> p (q j)"), "w", wq)
             multiply(acc[3, 1], 3, 3, t, codes[:], scales[:])
 
-        w2_q[2] = quantize_w2(w2_raw[2], "h")
+        w2_q[2] = quantize_w2(w2_raw[2], "w2_late")
         y2 = second_layer(w2_q[2], h_q[2])
-        w2_q[3] = quantize_w2(w2_raw[3])
-        h = hidden(hid.tile([P, C, PACK], BF16, name="h", align_bytes=64, bufs=1), relu_a[3], acc[3, 1])
-        y_sb = [hid.tile([N, C], F32, name="y_sb", bufs=2) for late in (2, 3)]
-        nc.vector.tensor_copy(y_sb[0][:], y2[:])
-        h_q[3] = quantize(h, "h", hid)
+        w2_grouped = hid.tile([P, N, PACK], BF16, name="w2_grouped", align_bytes=64, bufs=1)
+        interleave(w2_grouped[:], w2_raw[3], 0)
+        h = [behind(w2_start[2] + half * C * PACK, [P, C // 2, PACK], BF16, f"h3_{half}") for half in range(2)]
+        for half in range(2):
+            pairs_of_slots = slice(half * C // 4, (half + 1) * C // 4)
+            nc.vector.tensor_tensor(
+                h[half][:].rearrange("p (c r) t -> p c t r", r=2),
+                acc[3, 1][:].rearrange("p t (c r) -> p c t r", r=2)[:, pairs_of_slots],
+                relu_a[3, half][:],
+                MULT,
+            )
+        y_sb = [behind(start[last - 3], [N, C], F32, "y_sb2"), hid.tile([N, C], F32, name="y_sb3", bufs=1)]
+        nc.scalar.copy(y_sb[0][:], y2[:])
+        h_q[3] = (
+            hid.tile([P, C], U32, name="h_codes", align_bytes=64),
+            hid.tile([P, C], U8, name="h_scales", align_bytes=64),
+        )
+        for half in range(2):
+            slots = slice(half * C // 2, (half + 1) * C // 2)
+            nc.vector.quantize_mx(
+                out=h_q[3][0][:, slots].bitcast(FP8X4),
+                scales=h_q[3][1][:, slots],
+                in_=h[half][:].rearrange("p c t -> p (c t)"),
+            )
+            if half == 0:
+                w2_q[3] = quantize(w2_grouped[:].rearrange("p n j -> p (n j)"), "w2", hid)
         place(2, y_sb[0])
         nc.scalar.copy(y_sb[1][:], second_layer(w2_q[3], h_q[3])[:])
         place(3, y_sb[1])

@@ -186,8 +186,6 @@ def tile_moe_two_glu_relu_kernel(tc, xT, w1, w3, w2, gate, offs, dst, out):
         nc.sync.dma_start(offs_sb[:], offs)
         for s in range(1, PASSES):
             x_raw += load_passes(xT, s, 1)[0]
-        nc.sync.dma_start(dst_sb[:], dst)
-        nc.sync.dma_start(gate_row[:], gate[0:1, :].rearrange("o (n m) -> (o n) m", m=PACK))
         x_grouped = []
         for s in range(PASSES + 1):
             if s > 0:
@@ -198,10 +196,6 @@ def tile_moe_two_glu_relu_kernel(tc, xT, w1, w3, w2, gate, offs, dst, out):
             if s > 0:
                 gather(s - 1, 0)
 
-        bank = psum.tile([P, PACK, P], F32, name="turned", bufs=1)
-        for m in range(PACK):
-            nc.tensor.transpose(bank[:, m, :], gate_row[:, m : m + 1].to_broadcast([P, P]), ident[:])
-        nc.scalar.copy(gate_sb[:].rearrange("p (n m) -> p n m", m=PACK), bank[:].rearrange("p m n -> p n m"))
 
         steps = [(e, m, s) for e in range(E) for m in range(2) for s in range(PASSES)]
         last = len(steps) - 1
@@ -252,6 +246,14 @@ def tile_moe_two_glu_relu_kernel(tc, xT, w1, w3, w2, gate, offs, dst, out):
             start[c] = loaded_start
             if c == 2 * PASSES - 1:
                 w2_raw[0], w2_raw[1] = load_passes(w2[0:2].rearrange("e i n -> (e i) n"), 0, 2)[0]
+            if c == 0:
+                nc.sync.dma_start(gate_row[:], gate[0:1, :].rearrange("o (n m) -> (o n) m", m=PACK))
+                bank = psum.tile([P, PACK, P], F32, name="turned", bufs=1)
+                for part in range(PACK):
+                    nc.tensor.transpose(bank[:, part, :], gate_row[:, part : part + 1].to_broadcast([P, P]), ident[:])
+                nc.scalar.copy(gate_sb[:].rearrange("p (n m) -> p n m", m=PACK), bank[:].rearrange("p m n -> p n m"))
+            if c == 2:
+                nc.sync.dma_start(dst_sb[:], dst)
             if c > 0:
                 finish(c - 1)
             grouped[c] = wbf.tile([P, PACK, P, PACK], BF16, name="w_grouped", align_bytes=64)

@@ -25,7 +25,7 @@ W_VECTOR = 46
 W_VECTOR_END = 64
 BEFORE_LAST_VECTOR = 84
 FIRST_ROWS_VECTOR = 52
-LAST_VECTOR = (84, 76)
+LAST_VECTOR = (78, 64)
 GATHER = 256
 RING = 144 * 1024
 PAGE = 4096

from contextlib import ExitStack

import concourse.mybir as mybir
from concourse.masks import make_identity

K, T, E, C, H, N = 2048, 640, 4, 128, 512, 128
FLOPS = 2 * E * C * (2 * K * H + H * N)

F32 = mybir.dt.float32
BF16 = mybir.dt.bfloat16
U32 = mybir.dt.uint32
U16 = mybir.dt.uint16
U8 = mybir.dt.uint8
FP8X4 = mybir.dt.float8_e4m3fn_x4
RELU = mybir.ActivationFunctionType.Relu
MULT = mybir.AluOpType.mult

P = 128
PACK = 4
K_PASS = P * PACK
PASSES = K // K_PASS

X_VECTOR = 208
W_VECTOR = 46
W_VECTOR_END = 64
BEFORE_LAST_VECTOR = 84
FIRST_ROWS_VECTOR = 52
LAST_VECTOR = (78, 64)
GATHER = 256
RING = 144 * 1024
PAGE = 4096


def tile_moe_two_glu_relu_kernel(tc, xT, w1, w3, w2, gate, offs, dst, out):
    nc = tc.nc
    with ExitStack() as ctx:
        keep = ctx.enter_context(tc.tile_pool(name="keep", bufs=1))
        ring = ctx.enter_context(tc.tile_pool(name="ring", bufs=1))
        xbf = ctx.enter_context(tc.tile_pool(name="xbf", bufs=2))
        wbf = ctx.enter_context(tc.tile_pool(name="wbf", bufs=4))
        wq = ctx.enter_context(tc.tile_pool(name="wq", bufs=8))
        hid = ctx.enter_context(tc.tile_pool(name="hid", bufs=E))
        psum = ctx.enter_context(tc.psum_pool(name="psum", bufs=2))

        offs_sb = keep.tile([P, E * C // 16], U16, name="offs_sb")
        dst_sb = keep.tile([P, E * C // 16], U16, name="dst_sb")
        ident = keep.tile([P, P], F32, name="ident")
        make_identity(nc, ident[:])
        out_sb = keep.tile([P, T], F32, name="out_sb", align_bytes=256)
        nc.gpsimd.memset(out_sb[:], 0.0)
        gate_row = keep.tile([P, PACK], F32, name="gate_row")
        gate_sb = keep.tile([P, E * C], F32, name="gate_sb")
        all_codes = [keep.tile([P, T], U32, name=f"all_codes{s}", align_bytes=64) for s in range(PASSES)]
        all_scales = keep.tile([P, T], U8, name="all_scales", align_bytes=64)
        slot_codes = [keep.tile([P, E * C], U32, name=f"slot_codes{s}", align_bytes=64) for s in range(PASSES)]
        slot_scales = keep.tile([P, E * C], U8, name="slot_scales", align_bytes=64)
        nc.gpsimd.memset(all_scales[:], 0)

        ends = [0]

        def load(rows):
            size = -(-4 * rows.shape[1] * rows.shape[2] // PAGE) * PAGE
            start = ends[-1] if ends[-1] + size <= RING else 0
            ends.append(start + size)
            raw = ring.tile(list(rows.shape), F32, name=f"raw{len(ends)}", offset=start, align_bytes=PAGE)
            nc.sync.dma_start(raw[:], rows)
            return raw, start

        def load_passes(matrix, s0, count):
            rows = matrix[s0 * K_PASS : (s0 + count) * K_PASS, :]
            raw, start = load(rows.rearrange("(s p j) i -> p s (j i)", p=P, j=PACK))
            return [raw[:, s, :].rearrange("p (j i) -> p j i", j=PACK) for s in range(count)], start

        def load_rows(matrix, s, j0, j1):
            rows = matrix[s * K_PASS : (s + 1) * K_PASS, :].rearrange("(p j) i -> p j i", j=PACK)
            return load(rows[:, j0:j1, :])[0][:]

        def behind(start, shape, dtype, name):
            return ring.tile(shape, dtype, name=name, offset=start, align_bytes=256)

        def interleave(grouped, raw, share):
            rows = raw.rearrange("p j (g i) -> p g j i", i=PACK)
            into = grouped.rearrange("p (g i) j -> p g j i", i=PACK)
            nc.scalar.copy(into[:, share:], rows[:, share:])
            if share:
                nc.vector.tensor_copy(into[:, :share], rows[:, :share])

        def interleave_w(grouped, raw, share):
            rows = raw.rearrange("p j (q u r) -> p u q j r", u=2, r=2)
            into = grouped.rearrange("p (u r) q j -> p u q j r", u=2)
            nc.scalar.copy(into[:, :, share:], rows[:, :, share:])
            nc.vector.tensor_copy(into[:, :, :share], rows[:, :, :share])

        def quantize(values, name, pool):
            width = values.shape[1] // PACK
            codes = pool.tile([P, width], U32, name=name + "_codes", align_bytes=64)
            scales = pool.tile([P, width], U8, name=name + "_scales", align_bytes=64)
            nc.vector.quantize_mx(out=codes[:].bitcast(FP8X4), scales=scales[:], in_=values)
            return codes, scales

        def multiply(acc, e, s, t, codes, scales):
            slots = slice(e * C, (e + 1) * C)
            nc.tensor.matmul_mx(
                out=acc[:, t, :],
                lhsT=codes.bitcast(FP8X4),
                lhsT_scale=scales,
                rhs=slot_codes[s][:, slots].bitcast(FP8X4),
                rhs_scale=slot_scales[4 * s :, slots],
                start=s == 0 and t == 0,
                stop=s == PASSES - 1 and t == PACK - 1,
            )

        def first_layer(acc, e, s, grouped):
            codes, scales = quantize(grouped[:].rearrange("p t q j -> p (t q j)"), "w", wq)
            for t in range(PACK):
                cols = slice(t * P, (t + 1) * P)
                multiply(acc, e, s, t, codes[:, cols], scales[:, cols])

        def first_layer_early(acc, e, s, grouped):
            codes, scales = quantize(grouped[:].rearrange("p t q j -> p (t q j)"), "w", wq)
            slots = slice(e * C, (e + 1) * C)
            nc.tensor.matmul_mx(
                out=acc[:].rearrange("p t c -> p (t c)"),
                lhsT=slot_codes[s][:, slots].bitcast(FP8X4),
                lhsT_scale=slot_scales[4 * s :, slots],
                rhs=codes[:].bitcast(FP8X4),
                rhs_scale=scales[:],
                start=s == 0,
                stop=s == PASSES - 1,
            )

        def hidden_early(h, a_sb, acc):
            turned = psum.tile([P, 2, P], F32, name="turned", bufs=1)
            nc.vector.tensor_tensor(
                h[:].rearrange("p (u q r) -> p q u r", u=2, r=2),
                acc[:].rearrange("p t (g u r) -> p (t g) u r", u=2, r=2),
                a_sb[:].rearrange("p (q u r) -> p q u r", u=2, r=2),
                MULT,
            )
            words = h[:].bitcast(F32)
            for u in range(2):
                nc.tensor.transpose(turned[:, u, :], words[:, u * P : (u + 1) * P], ident[:])
            return turned

        def quantize_w2(raw, name="w2_grouped"):
            grouped = hid.tile([P, N, PACK], BF16, name=name, align_bytes=64, bufs=1)
            interleave(grouped[:], raw, 0)
            return quantize(grouped[:].rearrange("p n j -> p (n j)"), "w2", hid)

        def second_layer(w2_q, h_q):
            y = psum.tile([N, C], F32, name="y")
            nc.tensor.matmul_mx(
                out=y[:],
                lhsT=w2_q[0][:].bitcast(FP8X4),
                lhsT_scale=w2_q[1][:],
                rhs=h_q[0][:].bitcast(FP8X4),
                rhs_scale=h_q[1][:],
                start=True,
                stop=True,
            )
            return y

        def place(e, y_sb):
            idx = slice(e * C // 16, (e + 1) * C // 16)
            nc.vector.tensor_tensor(
                out_sb[:].indirect(dst_sb[:, idx]), y_sb[:], gate_sb[:, e * C : (e + 1) * C], MULT
            )

        def gather(s, g):
            cols = slice(g * GATHER, (g + 1) * GATHER)
            idx = slice(g * GATHER // 16, (g + 1) * GATHER // 16)
            nc.vector.tensor_copy(slot_codes[s][:, cols], all_codes[s][:].indirect(offs_sb[:, idx]))
            if s == PASSES - 1:
                nc.vector.tensor_copy(slot_scales[:, cols], all_scales[:].indirect(offs_sb[:, idx]))

        def quantize_x(s, grouped):
            flat = grouped[:].rearrange("p t j -> p (t j)")
            for a, b in ((0, 512), (512, T)):
                nc.vector.quantize_mx(
                    out=all_codes[s][:, a:b].bitcast(FP8X4),
                    scales=all_scales[4 * s :, a:b],
                    in_=flat[:, a * PACK : b * PACK],
                )

        x_raw = load_passes(xT, 0, 1)[0]
        nc.sync.dma_start(offs_sb[:], offs)
        for s in range(1, PASSES):
            x_raw += load_passes(xT, s, 1)[0]
        x_grouped = []
        for s in range(PASSES + 1):
            if s > 0:
                quantize_x(s - 1, x_grouped[s - 1])
            if s < PASSES:
                x_grouped.append(xbf.tile([P, T, PACK], BF16, name="x_grouped", align_bytes=64))
                interleave(x_grouped[s][:], x_raw[s], X_VECTOR // PACK)
            if s > 0:
                gather(s - 1, 0)


        steps = [(e, m, s) for e in range(E) for m in range(2) for s in range(PASSES)]
        last = len(steps) - 1
        acc, relu_a, turned, h_q, w2_raw, w2_q, grouped, start = {}, {}, {}, {}, {}, {}, {}, {}

        def finish(c):
            e, m, s = steps[c]
            if s == 0:
                acc[e, m] = psum.tile([P, PACK, C], F32, name=("acc_a", "acc_b")[m])
            (first_layer if c > last - PASSES else first_layer_early)(acc[e, m], e, s, grouped.pop(c))
            if e == 0 and m == 1:
                gather(s, 1)
            if e < E - 1 and m == 1 and s == 1:
                relu_a[e] = behind(start[c - 1], [C, H], F32, f"relu_a{e}")
                nc.scalar.activation(relu_a[e][:], acc[e, 0][:].rearrange("p t c -> p (t c)"), RELU)
            if e == E - 1 and m == 1 and s == 0:
                a_sb = behind(start[c - 1], [C, PACK, P], F32, "a_by_sets")
                nc.scalar.copy(a_sb[:], acc[e, 0][:].rearrange("p t (g u) -> p u (t g)", u=PACK))
                turned[e] = psum.tile([P, PACK, C], F32, name="turned", bufs=1)
                for t in range(PACK):
                    nc.tensor.transpose(turned[e][:, t, :], a_sb[:, t, :], ident[:])
            if e == E - 1 and m == 1 and s == 1:
                relu_start = [start[c - 1] + half * 2 * H for half in range(2)]
                by_pairs = turned[e][:].rearrange("p t (c r) -> p c t r", r=2)
                for half in range(2):
                    relu_a[e, half] = behind(relu_start[half], [P, C // 4, PACK, 2], F32, f"relu_a{e}_{half}")
                    nc.scalar.activation(relu_a[e, half][:], by_pairs[:, half * C // 4 : (half + 1) * C // 4], RELU)
            if e > 0 and m == 0 and s == 1:
                h = behind(start[c - 1], [C, H], BF16, f"h{e - 1}")
                turned[e - 1] = hidden_early(h, relu_a[e - 1], acc[e - 1, 1])
            if e > 0 and m == 0 and s == 3:
                regrouped = behind(start[c - 1], [P, C * PACK], BF16, f"h_grouped{e - 1}")
                words = regrouped[:].bitcast(F32).rearrange("p (c u) -> p c u", u=2)
                nc.scalar.copy(words, turned[e - 1][:].rearrange("p u c -> p c u"))
                h_q[e - 1] = quantize(regrouped[:], "h", hid)
            if e in (1, 2) and m == 0 and s == 3:
                w2_q[e - 1] = quantize_w2(w2_raw[e - 1])
            if e in (1, 2) and m == 1 and s == 1:
                y_sb = behind(start[c - 1] + 4 * H, [N, C], F32, f"y_sb{e - 1}")
                nc.scalar.copy(y_sb[:], second_layer(w2_q[e - 1], h_q[e - 1])[:])
                place(e - 1, y_sb)

        for c, (e, m, s) in enumerate(steps[:last]):
            w = (w1, w3)[m][e]
            count = 2 if e < E - 1 else 1
            if s % count == 0:
                loaded, loaded_start = load_passes(w, s, count)
            start[c] = loaded_start
            if c == 2 * PASSES - 1:
                w2_raw[0], w2_raw[1] = load_passes(w2[0:2].rearrange("e i n -> (e i) n"), 0, 2)[0]
            if c == 0:
                nc.sync.dma_start(gate_row[:], gate[0:1, :].rearrange("o (n m) -> (o n) m", m=PACK))
                bank = psum.tile([P, PACK, P], F32, name="turned", bufs=1)
                for part in range(PACK):
                    nc.tensor.transpose(bank[:, part, :], gate_row[:, part : part + 1].to_broadcast([P, P]), ident[:])
                nc.scalar.copy(gate_sb[:].rearrange("p (n m) -> p n m", m=PACK), bank[:].rearrange("p m n -> p n m"))
            if c == 2:
                nc.sync.dma_start(dst_sb[:], dst)
            if c > 0:
                finish(c - 1)
            grouped[c] = wbf.tile([P, PACK, P, PACK], BF16, name="w_grouped", align_bytes=64)
            if c <= last - PASSES:
                interleave(grouped[c][:].rearrange("p t q j -> p (t q) j"), loaded[s % count], W_VECTOR)
            else:
                interleave_w(grouped[c][:], loaded[0], BEFORE_LAST_VECTOR if c == last - 1 else W_VECTOR_END)

        pairs = [load_rows(w3[3], 3, j, j + 2) for j in (0, 2)]
        w2_start = {}
        for late in (2, 3):
            (w2_raw[late],), w2_start[late] = load_passes(w2[late], 0, 1)
        finish(last - 1)
        final = wbf.tile([P, PACK, P, PACK], BF16, name="w_grouped", align_bytes=64)
        interleave_w(final[:, :, :, 0:2], pairs[0], FIRST_ROWS_VECTOR)
        rows = pairs[1].rearrange("p j (q u r) -> p u q j r", u=2, r=2)
        into = final[:, :, :, 2:4].rearrange("p (u r) q j -> p u q j r", u=2)
        for u in range(2):
            nc.scalar.copy(into[:, u, LAST_VECTOR[u] :], rows[:, u, LAST_VECTOR[u] :])
            nc.vector.tensor_copy(into[:, u, : LAST_VECTOR[u]], rows[:, u, : LAST_VECTOR[u]])
        for t in range(PACK):
            codes, scales = quantize(final[:, t].rearrange("p q j -> p (q j)"), "w", wq)
            multiply(acc[3, 1], 3, 3, t, codes[:], scales[:])

        w2_q[2] = quantize_w2(w2_raw[2], "w2_late")
        y2 = second_layer(w2_q[2], h_q[2])
        w2_grouped = hid.tile([P, N, PACK], BF16, name="w2_grouped", align_bytes=64, bufs=1)
        interleave(w2_grouped[:], w2_raw[3], 0)
        h = [behind(w2_start[2] + half * C * PACK, [P, C // 2, PACK], BF16, f"h3_{half}") for half in range(2)]
        for half in range(2):
            pairs_of_slots = slice(half * C // 4, (half + 1) * C // 4)
            nc.vector.tensor_tensor(
                h[half][:].rearrange("p (c r) t -> p c t r", r=2),
                acc[3, 1][:].rearrange("p t (c r) -> p c t r", r=2)[:, pairs_of_slots],
                relu_a[3, half][:],
                MULT,
            )
        y_sb = [behind(start[last - 3], [N, C], F32, "y_sb2"), hid.tile([N, C], F32, name="y_sb3", bufs=1)]
        nc.scalar.copy(y_sb[0][:], y2[:])
        h_q[3] = (
            hid.tile([P, C], U32, name="h_codes", align_bytes=64),
            hid.tile([P, C], U8, name="h_scales", align_bytes=64),
        )
        for half in range(2):
            slots = slice(half * C // 2, (half + 1) * C // 2)
            nc.vector.quantize_mx(
                out=h_q[3][0][:, slots].bitcast(FP8X4),
                scales=h_q[3][1][:, slots],
                in_=h[half][:].rearrange("p c t -> p (c t)"),
            )
            if half == 0:
                w2_q[3] = quantize(w2_grouped[:].rearrange("p n j -> p (n j)"), "w2", hid)
        place(2, y_sb[0])
        nc.scalar.copy(y_sb[1][:], second_layer(w2_q[3], h_q[3])[:])
        place(3, y_sb[1])

        nc.sync.dma_start(out, out_sb[:])
